import numpy as np, ml_dtypes
CORES = [6,15,38,47]
N = 4
BF = ml_dtypes.bfloat16
S, L, CAP, RO, KM = 4096, 256, 64, 6, 3967
W = S + RO * CAP
def joined(c, T):
    e = np.add.accumulate(4 + (c & 3), axis=1)
    j = np.minimum(np.sum(e[:, :, None] <= (5 * np.arange(L) + 2)[None, None, :], axis=1), L - 2)
    p = np.take_along_axis(c, j, 1); q = np.take_along_axis(c, j + 1, 1)
    left = np.take_along_axis(T, p[:, None, :], 2)[:, 8:]; right = np.take_along_axis(T, q[:, None, :], 2)[:, :8]
    return p, np.concatenate([left, right], axis=1).astype(np.int64)
def places(z, w, k):
    u = np.sum(z * w[:, :, 0:1], axis=1) & (S - 1); v = np.sum(z * w[:, :, 1:2], axis=1) & (S - 1)
    return (((u * v) >> 5)[:, None, :] + k[:, :, None] * u[:, None, :]) & (S - 1)
def probe(z, w, k, b, U):
    h = places(z, w, k)
    d = np.stack([np.sum(np.abs(np.take_along_axis(U, h[:, m:m + 1], 2) - z), axis=1) for m in range(16)], axis=1)
    m = np.argmin(d, axis=1)[:, None, :]
    return np.take_along_axis(h, m, 1)[:, 0], np.take_along_axis(d, m, 1)[:, 0] < b[:, None]
def lowest(h, fit):
    win = np.zeros(fit.shape, bool)
    for g in range(8):
        i = np.flatnonzero(fit[g]); win[g, i[np.unique(h[g, i], return_index=True)[1]]] = True
    return win
def parts(rng):
    return (rng.integers(0, 256, (N, 8, 16, S), dtype=np.int16), rng.integers(0, 256, (N, 8, 16, S), dtype=np.int16), rng.integers(0, S, (N, 8, L)),
            rng.integers(0, 4096, (N, 8, 16, 2)), rng.integers(0, KM + 1, (N, 8, 16)), rng.integers(840, 1040, (N, 8)))
def pack(us, tp, c, w, k, th):
    return {"us": us.reshape(N, 128, S).astype(np.float32).astype(BF), "tp": tp.reshape(N, 128, S).astype(np.float32).astype(BF), "c0": np.ascontiguousarray(c).astype(np.int32),
            "hw": np.ascontiguousarray(w.reshape(N, 128, 2)).astype(np.int32), "km": np.ascontiguousarray(k.reshape(N, 128, 1)).astype(np.int32), "th": np.ascontiguousarray(th.reshape(N, 8, 1)).astype(np.int32)}
def setup_inputs(rng):
    return pack(*parts(rng))
def near(z, d):
    a = d[None, :] // 16 + (np.arange(16)[:, None] < d[None, :] % 16)
    return np.where(z < 128, z + a, z - a)
def setup_inputs_corners(rng):
    us, tp, c, w, k, th = parts(rng); w[:, :, 0, 0] |= 1; cnt = (0, 1, CAP - 1, CAP, CAP + 1, L); used = {}; sent = {}; zs = []
    def plant(q, g, h, z, todo):
        st, sl, ds = [], [], []
        for i, d in todo:
            r = int(rng.integers(0, 16)); cand = h[:, i].tolist()
            for m in range(16):
                s = cand[(m + r) % 16]
                if s not in used[q, g]:
                    used[q, g].add(s); st.append(s); sl.append(i); ds.append(d); break
        if st: us[q, g][:, np.array(st)] = near(z[:, np.array(sl)], np.array(ds))
    for q in range(N):
        for g in range(8):
            v = (g + q) % 8; used[q, g] = set()
            if v == 6: c[q, g] = 4 * rng.integers(0, S // 4, L) + 3; c[q, g, :3] = S - 1
            elif v == 7: c[q, g] = 4 * rng.integers(0, S // 4, L); c[q, g, L - 3:] = 0
            else: c[q, g] = 4 * rng.permutation(S // 4)[:L] + 1; k[q, g] = rng.permutation(min(S, KM + 1))[:16]; th[q, g] = rng.choice(np.array([1, 2, 64, 100]))
            if v in (1, 2, 3): us[q, g, :, 0] = 0; used[q, g].add(0)
        p, z = joined(c[q], tp[q]); even = (np.sum(z * w[q, :, :, 0:1], axis=1) & 1) == 0
        for g in range(8):
            if (g + q) % 8 < 6: tp[q, g, 8, np.unique(p[g, even[g]])] ^= 1
        p, z = joined(c[q], tp[q]); zs.append(z); h = places(z, w[q], k[q])
        for g in range(8):
            v = (g + q) % 8
            if v > 5: continue
            n = cnt[v]; pair = 2 if n >= 2 else 0; front = rng.permutation(L - 2).tolist(); t = int(th[q, g])
            poor = front[:n - pair] + ([L - 2, L - 1] if pair else []); fits = front[n - pair:] + ([] if pair else [L - 2])
            plant(q, g, h[g], z[g], [(i, (t - 1) * int(rng.integers(0, 2))) for i in fits] + [(i, t) for i in poor if i < L - 1 and rng.random() < 0.5])
            sent[q, g] = sorted(poor)[:CAP]
    for q in range(N):
        a = (q + 1) % N; h = places(zs[q], w[a], k[a])
        for g in range(8):
            if (q, g) in sent:
                t = int(th[a, g]); full = (g + q) % 8 == 4
                plant(a, g, h[g], zs[q][g], [(i, (0, t - 1, t)[int(rng.integers(0, 2 if full else 3))]) for i in sent[q, g] if i < L - 1 and (full or rng.random() < 0.6)])
    return pack(us, tp, c, w, k, th)
def setup_inputs_ends(rng):
    us = 255 * rng.integers(0, 2, (N, 8, 16, S), dtype=np.int16); tp = 255 * rng.integers(0, 2, (N, 8, 16, S), dtype=np.int16)
    inner = np.argsort(rng.random((N, 8, L)), axis=-1) < 5 * L // 16; anyc = rng.integers(0, S, (N, 8, L)); roll = rng.random((N, 8, L))
    w = 4095 * rng.integers(0, 2, (N, 8, 16, 2)); w[:, :, 0, 0] = 0; w[:, :, 1, 0] = 4095
    k = np.where(np.argsort(rng.random((N, 8, 16)), axis=-1) < 4, rng.integers(0, KM + 1, (N, 8, 16)), KM * rng.integers(0, 2, (N, 8, 16)))
    th = np.stack([4080 * (rng.permutation(8) % 2) for q in range(N)]); big = np.stack([rng.permutation(8) < 4 for q in range(N)]); big[:, 7] = True; big[0, 0] = True
    if th[N - 1, 7] == 0: th[N - 1, int(np.argmax(th[N - 1]))] = 0; th[N - 1, 7] = 4080
    c = np.where(inner, anyc, (S - 1) * (roll < 0.5)); base = ((S - 1) ** 2 >> 5) & (S - 1); one = np.zeros(16, np.int16); one[0] = 1
    for q in range(N):
        for g in range(8):
            if not big[q, g]: continue
            w[q, g] = 4095; us[q, g, :, 0] = 255; tp[q, g, :, 0] = 255; tp[q, g, :, S - 1] = 0; tp[q, g, :, S - 2] = 0; tp[q, g, 8, S - 2] = 1
            far = (S - 1, 1, 2) if g == 7 or rng.random() < 0.5 else (2, S - 1, 1)
            for lane, s in zip((1, 14, 15), far): k[q, g, lane] = (base - s) & (S - 1); us[q, g, :, s] = one
            k[q, g, 0] = 0; k[q, g, 2] = KM
            c[q, g] = np.where(inner[q, g], anyc[q, g] // 4 * 4, (S - 1) * (roll[q, g] < 0.2))
            if rng.random() < 0.5: c[q, g, 0] = S - 2; c[q, g, 1] = S - 1
            c[q, g, 4:6] = S - 1; c[q, g, 6:9] = 0; c[q, g, L - 2] = S - 2; c[q, g, L - 1] = S - 1
    return pack(us, tp, c, w, k, th)
def setup_inputs_refuse(rng):
    d = setup_inputs_ends(rng); d["th"][1] = 0
    return d
def setup_inputs_spread(rng):
    us, tp, c, w, k, th = parts(rng)
    def stones():
        v = np.floor(np.exp2(8 * rng.random((N, 8, 1, S), dtype=np.float32)) * rng.random((N, 8, 16, S), dtype=np.float32)).astype(np.int16)
        v = np.minimum(v, 255); return np.where(rng.random((N, 8, 1, S)) < 0.25, 255 - v, v)
    c = np.minimum((S * rng.random((N, 8, L)) ** 3).astype(np.int64), S - 1); c[:, ::2] = S - 1 - c[:, ::2]
    w = np.minimum(np.exp2(12.01 * rng.random((N, 8, 16, 2))).astype(np.int64) - (rng.random((N, 8, 16, 2)) < 0.05), 4095)
    k = np.maximum(np.minimum(np.exp2(12 * rng.random((N, 8, 16))).astype(np.int64) - 1, KM), 0)
    th = np.where(rng.random((N, 8)) < 0.25, rng.integers(0, 4081, (N, 8)), np.exp2(6 + 4 * rng.random((N, 8))).astype(np.int64))
    us = stones(); tp = stones()
    for q in range(N):
        g = int(rng.integers(0, 8))
        us[q, g] = rng.integers(0, 8, (16, S)); us[q, g, 0] += 248
        tp[q, g] = rng.integers(248, 256, (16, S)); tp[q, g, 8] = rng.integers(0, 2, S)
        w[q, g, :, 0] = 3072; w[q, g, 0, 0] = 4095; w[q, g, :, 1] = rng.integers(0, 4096, 16)
        k[q, g] = rng.permutation(KM + 1)[:16]; th[q, g] = 4080
    return pack(us, tp, c, w, k, th)
def setup_inputs_ties(rng):
    us, tp, c, w, k, th = parts(rng); flat = int(rng.integers(0, 8)); z = np.full((1, 16, 1), 255); z[0, 0] = 0
    for q in range(N):
        for g in range(8):
            pr = rng.integers(0, 256, (16, 12)); tp[q, g] = pr[:, rng.integers(0, 12, S)]
            us[q, g, :8] = pr[8:, rng.integers(0, 12, S)]; us[q, g, 8:] = pr[:8, rng.integers(0, 12, S)]
            th[q, g] = int(rng.choice(np.array([1, 400, 600, 700, 900])))
        us[q, flat] = 0; us[q, flat, 0] = 255; tp[q, flat] = 255; tp[q, flat, 8] = 0; th[q, flat] = 4080
        w[q, flat, 1, 0] ^= 1 - int(np.sum(w[q, flat, 1:, 0])) % 2
        if places(z, w[q, flat][None], k[q, flat][None])[0, 0, 0] == 0: k[q, flat, 0] ^= 1
    return pack(us, tp, c, w, k, th)
def check_inputs(d):
    bad = []
    for a, lo, hi in (("us", 0, 255), ("tp", 0, 255), ("c0", 0, S - 1), ("hw", 0, 4095), ("km", 0, KM), ("th", 0, 4080)):
        v = np.asarray(d[a]).astype(np.float64)
        if not (np.min(v) >= lo and np.max(v) <= hi): bad.append("range of " + a)
        elif np.any(v != np.floor(v)): bad.append("whole numbers in " + a)
    return bad
def reference(us, tp, c0, hw, km, th):
    U = np.zeros((N, 8, 16, W), np.int64); U[..., :S] = us.astype(np.float32).astype(np.int64).reshape(N, 8, 16, S)
    T = np.zeros((N, 8, 16, W), np.int64); T[..., :S] = tp.astype(np.float32).astype(np.int64).reshape(N, 8, 16, S)
    C = c0.astype(np.int64); w = hw.astype(np.int64).reshape(N, 8, 16, 2); k = km.astype(np.int64).reshape(N, 8, 16); t0 = th.astype(np.int64).reshape(N, 8)
    P = np.zeros(N, np.int64); out = []
    for t in range(RO):
        b = t0 + (P & 63)[:, None]; new, poor, zs = [], [], []
        for a in range(N):
            p, z = joined(C[a], T[a]); h, fit = probe(z, w[a], k[a], b[a], U[a]); win = lowest(h, fit)
            for g in range(8): U[a, g][:, h[g, win[g]]] = 255
            new.append(np.where(win, h, p)); poor.append(~fit); zs.append(z)
        for q in range(N):
            a = (q + 1 + t % (N - 1)) % N; sl = [np.flatnonzero(poor[q][g])[:CAP] for g in range(8)]
            z = np.zeros((8, 16, CAP), np.int64); use = np.zeros((8, CAP), bool)
            for g in range(8): z[g][:, :len(sl[g])] = zs[q][g][:, sl[g]]; use[g, :len(sl[g])] = True
            h, fit = probe(z, w[a], k[a], b[a], U[a]); win = lowest(h, fit & use)
            for g in range(8):
                s = np.flatnonzero(win[g]); n = h[g, s]; own = S + CAP * t + s
                U[q, g][:, own] = U[a, g][:, n]; T[q, g][:, own] = T[a, g][:, n]; U[a, g][:, n] = 255; new[q][g, sl[g][s]] = own
        P = np.array([int(np.sum(m)) for m in poor]); C = np.stack(new); out.append(C)
    return {"yc": np.concatenate(out, axis=2).astype(np.float32), "yu": U.reshape(N, 128, W).astype(np.float32).astype(BF)}

@@ -1,0 +1,620 @@
+import math
+from concourse.mybir import dt, AluOpType, AxisListType, ActivationFunctionType
+import comms_topo
+
+RO, L, S, CAP = 6, 256, 4096, 64
+UNF = -2048.0
+
+_B = {}
+
+
+def _b(name, cols, dtype, rows=128):
+    _B[name] = ("sbuf", [rows, cols], dtype)
+
+
+F, BF, H, I, U16 = "float32", "bfloat16", "float16", "int32", "uint16"
+_b("US", 4352, BF); _b("TP", 4096, BF)
+_b("c8", 256, I, 8); _b("hwi", 2, I); _b("kmi", 1, I); _b("th8", 1, I, 8)
+_b("c8h", 256, H, 8); _b("th8h", 1, H, 8); _b("hwf", 2, F); _b("hwg", 2, F); _b("hwh", 2, H); _b("wl", 2, F); _b("wr", 2, F); _b("ws", 2, F)
+_b("kh", 16, H); _b("KR", 16, F); _b("th16", 1, F); _b("b16a", 1, F); _b("b16b", 1, F); _b("ksc", 1, F)
+_b("IC", 256, I); _b("pI", 1, I); _b("sI", 1, I); _b("gI", 1, I); _b("s8I", 1, I); _b("s2I", 1, I)
+_b("pF", 1, F); _b("sF", 1, F); _b("gF", 1, F); _b("s8F", 1, F); _b("s2F", 1, F); _b("sge8", 1, F); _b("slt8", 1, F)
+_b("CS", 256, I); _b("CG", 256, I); _b("C3", 128, I); _b("CSB", 128, BF); _b("CQB", 128, BF); _b("tmpA", 128, F); _b("tmpB", 128, F)
+_b("MWR", 256, F); _b("RST", 256, F); _b("BLKH", 128, H); _b("BLKB", 128, BF); _b("ONEB", 128, BF); _b("IDH", 128, H); _b("IDB", 128, BF); _b("IDN", 128, BF); _b("EQM", 256, F)
+_b("TRIMB", 128, BF); _b("PL", 128, BF); _b("PR", 128, BF); _b("PH", 128, H); _b("SEL", 2048, BF); _b("REP8", 128, H, 8)
+_b("WT", 24 * 128, H); _b("MQ", 128, F); _b("MC", 256, F); _b("MCL", 64, F); _b("t256", 256, I); _b("TRP", 256, F)
+_b("C255", 256, BF); _b("T5", 256, F); _b("KONST", 256, BF); _b("one16", 16, F); _b("oneR", 256, H); _b("CC", 16, F); _b("JW0", 16, F); _b("jI", 16, I)
+_b("J256", 16, F); _b("D4096", 16, F); _b("FIX", 32, F); _b("CLf", 16, F); _b("CL", 16, U16); _b("IC64", 64, F); _b("PF64", 64, F); _b("CCL", 4, F)
+for _k in "01":
+    _b("CX" + _k, 640, F); _b("TX" + _k, 640, BF)
+_b("CM", 256, F); _b("CM2", 256, F); _b("CL0", 16, U16)
+_b("ZB", 256, BF); _b("UVM", 128, F); _b("UT", 64, F); _b("UVI", 32, I); _b("UVA", 32, I); _b("UVW", 16, I); _b("UQ", 32, F)
+_b("HV", 256, I); _b("HF", 64, F); _b("HI", 256, I); _b("HO", 256, U16); _b("HT", 768, F)
+_b("X", 4096, BF); _b("A", 4096, BF); _b("K", 256, F); _b("K2", 64, F); _b("K3", 64, F); _b("K5", 32, F); _b("K6", 32, F); _b("K7", 32, F); _b("KP", 128, F); _b("KQ", 64, F); _b("MP", 128, F); _b("ML", 128, F); _b("SLP", 1024, BF); _b("s3F", 1, F); _b("k2I", 128, I); _b("pz", 128, F); _b("kz1", 256, I); _b("kz2", 256, F); _b("C7B", 128, BF); _b("HN", 16, F); _b("HG", 16, F); _b("UR", 256, BF); _b("KEY", 16, F)
+_b("PO", 16, F); _b("PN", 16, BF); _b("SC", 16, BF); _b("UA", 16, F); _b("PEN", 16, H); _b("OF", 16, U16); _b("ZA", 768, BF)
+_b("PPI", 1, I); _b("PPJ", 1, I); _b("PPF", 1, F)
+_b("KI", 16, I); _b("MI", 16, I); _b("LA", 16, F); _b("LB", 16, F); _b("LC", 16, F); _b("LD", 16, F); _b("LL", 16, U16)
+_b("HM", 256, H); _b("HS", 256, F); _b("HRH", 256, H); _b("HRT", 256, F); _b("HW", 16, F); _b("HD", 16, F); _b("HL", 16, U16)
+_b("ET", 17 * 256, BF); _b("WN", 256, BF); _b("WM", 256, F); _b("WS", 256, F); _b("LO1", 16, F); _b("LO2", 16, F); _b("LO", 16, U16)
+_b("CI", 256, I); _b("CI3", 256, I); _b("W16", 256, H); _b("EE", 512, H); _b("FI", 32, I); _b("FB", 32, F); _b("FC", 32, F); _b("NW", 16, F); _b("UN0", 16, F); _b("UNC", 16, F)
+_b("EB", 16, F); _b("SG", 4096, BF); _b("RJ", 272, BF); _b("FIRST", 256, BF); _b("JW", 16, F); _b("JL", 16, U16); _b("FW", 256, BF); _b("JX", 16, F); _b("JL2", 16, U16)
+_b("EA", 768, F); _b("EM", 64, F); _b("EQ", 64, F); _b("FAI", 4, I); _b("FA", 4, F); _b("OB", 4, F); _b("OBU", 4, U16)
+for _k in range(RO):
+    _b("ZL%d" % _k, 64, BF); _b("RB%d" % _k, 136, BF)
+_b("ZT", 256, BF); _b("lUVM", 32, F); _b("lUT", 16, F); _b("lUVI", 8, I); _b("lUVA", 8, I); _b("lUVW", 4, I); _b("lUQ", 8, F)
+_b("lHV", 64, I); _b("lHI", 64, I); _b("lHO", 64, U16); _b("lHT", 128, F); _b("lX", 1024, BF); _b("lA", 1024, BF)
+_b("lK", 128, F); _b("lK0", 64, F); _b("lK1", 32, F); _b("lK2", 16, F); _b("lK3", 8, F); _b("lKEY", 4, F); _b("lKI", 4, I); _b("lMI", 4, I); _b("lPO", 4, F); _b("lLA", 4, F); _b("lLB", 4, F)
+_b("lLC", 4, F); _b("lLD", 4, F); _b("lLL", 4, U16); _b("lHM", 64, H); _b("lHS", 64, F); _b("lHRH", 64, H); _b("lHRT", 64, F); _b("lHW", 4, F); _b("lHD", 4, F); _b("lHL", 4, U16)
+_b("lET", 320, BF); _b("GR", 64, BF); _b("GM", 64, F); _b("GS", 64, F); _b("RS", 136, BF); _b("lO1", 4, F); _b("lO2", 4, F); _b("lLO", 4, U16)
+_PS = ["UVP", "ZP", "DA", "DB", "HR", "CT", "MS", "JP"]
+_SIZE = {F: 4, BF: 2, H: 2, I: 4, U16: 2}
+_OWN = ("US", "TP", "X", "A", "ZA")
+BYS = {3: "ZP", 12: "CT", 13: "ZP"}
+SCRATCH = {}
+_AT = {}
+_fill = {}
+for _n, (_w, _sh, _d) in _B.items():
+    if _n in _OWN or _n[:2] in ("ZL", "RB", "RS") or _sh[0] != 128:
+        SCRATCH[_n] = (_w, _sh, _d); _AT[_n] = (_n, 0)
+    else:
+        _q = 32 // _SIZE[_d]
+        _AT[_n] = ("ar_" + _d, _fill.get(_d, 0))
+        _fill[_d] = _fill.get(_d, 0) + (_sh[1] + _q - 1) // _q * _q
+for _d, _c in _fill.items():
+    SCRATCH["ar_" + _d] = ("sbuf", [128, _c], _d)
+for _n in _PS:
+    SCRATCH[_n] = ("psum", [128, 512], F); _AT[_n] = (_n, 0); _B[_n] = SCRATCH[_n]
+ND = 24
+SEMAPHORES = ["sV", "sS", "sP", "sG", "la", "lr"] + ["ask%d" % k for k in range(RO)] + ["rep%d" % k for k in range(RO)] + ["d%d" % k for k in range(ND)]
+
+CY = 0.001
+GA, SCT = 1.56, 3.8
+HOP, OWN = 0.10, 0.05
+FLIGHT = 2.6
+
+
+def build(rank, core, T, topo):
+    ops = []
+
+    def ap(name, lo=0, hi=None, st=1, rows=None):
+        hi = _B[name][1][1] if hi is None else hi
+        return ("a", name, lo, hi, st, rows)
+
+    def ind(win, off):
+        return ("i", win, off)
+
+    def ext(name, lo, hi):
+        return ("x", name, lo, hi)
+
+    def res(d):
+        if d[0] == "i":
+            return res(d[1]).indirect(res(d[2]))
+        if d[0] == "x":
+            return T[d[1]][:, d[2]:d[3]]
+        _, name, lo, hi, st, rows = d
+        t, off = _AT[name]
+        n = _B[name][1][0]
+        rs = slice(0, n) if rows is None else rows
+        return T[t][rs, off + lo:off + hi] if st == 1 else T[t][rs, off + lo:off + hi:st]
+
+    def acc(d):
+        if d[0] == "x":
+            return []
+        if d[0] == "i":
+            return acc(d[1]) + acc(d[2])
+        return [(d[1], d[2], d[3], d[4])]
+
+    def n_of(d):
+        return 16 * n_of(d[2]) if d[0] == "i" else (d[3] - d[2] + d[4] - 1) // d[4]
+
+    def size(d):
+        return _SIZE[_B[d[1]][2]]
+
+    def isps(d):
+        return d[0] == "a" and d[1] in _PS
+
+    def put(q, fn, reads, writes, cost, sem=None, inc=1):
+        R, W = [], []
+        for d in reads:
+            R += acc(d)
+        for d in writes:
+            if d[0] == "i":
+                W += acc(d[1]); R += acc(d[2])
+            else:
+                W += acc(d)
+        ops.append({"q": q, "fn": fn, "R": R, "W": W, "c": cost, "sem": sem, "inc": inc})
+
+    class V:
+        pass
+
+    from_ops = AluOpType
+
+    def vcost(n, full, inds, outs_ind):
+        if outs_ind:
+            return 0.06 + n * SCT * CY
+        if inds:
+            return 0.06 + n * GA * CY
+        return max(64, n * full) * CY
+
+    def sc(x):
+        return res(x) if isinstance(x, tuple) else x
+
+    def tt(o, a, b, op):
+        full = 1 if isps(a) or isps(b) else 2
+        put("V", lambda g: g.vector.tensor_tensor(res(o), res(a), res(b), op), [a, b], [o], vcost(n_of(o), full, a[0] == "i", o[0] == "i"))
+
+    def ts(o, a, s1, op0, s2=None, op1=None):
+        two = 0.5 if not isps(a) and not isps(o) and o[0] == "a" and size(a) == 2 and size(o) == 2 else 1
+        rd = [a] + [x for x in (s1, s2) if isinstance(x, tuple)]
+        if op1 is None:
+            put("V", lambda g: g.vector.tensor_scalar(res(o), res(a), sc(s1), None, op0), rd, [o], vcost(n_of(o), two, a[0] == "i", o[0] == "i"))
+        else:
+            put("V", lambda g: g.vector.tensor_scalar(res(o), res(a), sc(s1), sc(s2), op0, op1), rd, [o], vcost(n_of(o), two, a[0] == "i", o[0] == "i"))
+
+    def cp(o, a):
+        two = 0.5 if a[0] == "a" and o[0] == "a" and not isps(a) and size(a) == 2 and size(o) == 2 else 1
+        put("V", lambda g: g.vector.tensor_copy(res(o), res(a)), [a], [o], vcost(n_of(o), two, a[0] == "i", o[0] == "i"))
+
+    def scan(o, a, b):
+        put("V", lambda g: g.vector.tensor_tensor_scan(res(o), res(a), res(b), 0.0, MUL, ADD), [a, b], [o], vcost(n_of(o), 1, False, False))
+
+    def fill(o, v):
+        put("V", lambda g: g.vector.memset(res(o), v), [], [o], vcost(n_of(o), 0.5, False, False))
+
+    def act(o, a, func, bias=0.0, scale=1.0):
+        rd = [a] + [x for x in (bias, scale) if isinstance(x, tuple)]
+        put("S", lambda g: g.scalar.activation(res(o), res(a), func, bias=sc(bias), scale=sc(scale)), rd, [o],
+            0.08 + n_of(o) * (GA if a[0] == "i" else 1) * CY)
+
+    def mm(lst):
+        def fn(g):
+            r = None
+            for o, l, rh, st, sp in lst:
+                r = g.tensor.matmul(res(o), res(l), res(rh), st, sp)
+            return r
+        put("P", fn, [x[1] for x in lst] + [x[2] for x in lst], [x[0] for x in lst], sum(max(64, n_of(x[2])) for x in lst) * CY)
+
+    def later(k):
+        ops[-1].setdefault("after", []).append(k)
+
+    nd = [0]
+
+    def dma(o, a, cost):
+        k = "d%d" % nd[0]; nd[0] += 1
+        put("Y", lambda g: g.sync.dma_start(res(o) if isinstance(o, tuple) else o, res(a) if isinstance(a, tuple) else a),
+            [a] if isinstance(a, tuple) else [], [o] if isinstance(o, tuple) else [], cost, sem=k, inc=16)
+
+    ADD, SUB, MUL, MIN, MAX = from_ops.add, from_ops.subtract, from_ops.mult, from_ops.min, from_ops.max
+    EQ, NE, GE, GT, LT, LE = from_ops.is_equal, from_ops.not_equal, from_ops.is_ge, from_ops.is_gt, from_ops.is_lt, from_ops.is_le
+    SHR, AND = from_ops.arith_shift_right, from_ops.bitwise_and
+    AF = ActivationFunctionType
+
+    dma(ap("c8"), T.c0[:, :], 2.0); dma(ap("hwi"), T.hw[:, :], 2.0); dma(ap("kmi"), T.km[:, :], 2.0); dma(ap("th8"), T.th[:, :], 2.0)
+    dma(ap("TP"), ext("tp", 0, 4096), 6.0)
+    for k in range(4):
+        later(k)
+    dma(ap("US", 0, 4096), ext("us", 0, 4096), 8.0); later(4)
+
+    put("G", lambda g: g.iota(res(ap("pI")), [[0, 1]], 0, 1), [], [ap("pI")], 0.2)
+    put("G", lambda g: g.iota(res(ap("IC")), [[1, 256]], 0, 0), [], [ap("IC")], 0.6)
+    ts(ap("sI"), ap("pI"), 15, AND); ts(ap("gI"), ap("pI"), 4, SHR); ts(ap("s2I"), ap("sI"), 2, SHR)
+    ts(ap("s8I"), ap("pI"), 8, ADD); ts(ap("s8I"), ap("s8I"), 15, AND)
+    for a, b in (("pF", "pI"), ("sF", "sI"), ("gF", "gI"), ("s8F", "s8I"), ("s2F", "s2I")):
+        cp(ap(a), ap(b))
+    ts(ap("sge8"), ap("sF"), 7.5, GT); ts(ap("slt8"), ap("sF"), 7.5, LT)
+    ts(ap("CS"), ap("IC"), 15, AND); ts(ap("CG"), ap("IC"), 4, SHR); ts(ap("C3"), ap("IC", 0, 128), 3, AND)
+    ts(ap("BLKB"), ap("CG", 0, 128), ap("gF"), EQ); cp(ap("BLKH"), ap("BLKB"))
+    r8 = slice(0, 8)
+    ts(ap("REP8"), ap("CG", 0, 128, 1, r8), ap("pF", 0, 1, 1, r8), EQ)
+    ts(ap("tmpA"), ap("C3"), 1.0, ADD); tt(ap("tmpB"), ap("tmpA"), ap("BLKB"), MUL); ts(ap("CQB"), ap("tmpB"), -1.0, ADD)
+    ts(ap("tmpA"), ap("CS", 0, 128), 1.0, ADD); tt(ap("tmpB"), ap("tmpA"), ap("BLKB"), MUL); ts(ap("CSB"), ap("tmpB"), -1.0, ADD)
+    ts(ap("PH"), ap("CSB"), ap("s8F"), EQ)
+    ts(ap("PL"), ap("CSB"), ap("s8F"), EQ, ap("sge8"), MUL); ts(ap("PR"), ap("CSB"), ap("s8F"), EQ, ap("slt8"), MUL)
+    cp(ap("hwf"), ap("hwi")); ts(ap("hwg"), ap("hwf"), 2047.5, GT, -4096.0, MUL); tt(ap("hwg"), ap("hwf"), ap("hwg"), ADD); cp(ap("hwh"), ap("hwg"))
+    mm([(ap("MS", 0, 2), ap("PH"), ap("hwh"), True, True)])
+    cp(ap("ws"), ap("MS", 0, 2)); ts(ap("wl"), ap("ws"), ap("sge8"), MUL); ts(ap("wr"), ap("ws"), ap("slt8"), MUL)
+
+    def wt(k, qv, r):
+        i = (k * 2 + qv) * 4 + r
+        return ap("WT", i * 128, i * 128 + 128)
+    for k, nm in enumerate(("wl", "wr", "hwg")):
+        for qv in (0, 1):
+            for r in range(4):
+                ts(wt(k, qv, r), ap("CQB"), float(r), EQ, ap(nm, qv, qv + 1), MUL)
+    ts(ap("MQ"), ap("C3"), ap("s2F"), EQ)
+    ts(ap("MWR"), ap("CS"), ap("sF"), EQ); ts(ap("RST"), ap("CS"), 0.5, GT)
+    ts(ap("ksc"), ap("kmi"), -2048.0, ADD); ts(ap("kh"), ap("CS", 0, 16), ap("sF"), EQ, ap("ksc"), MUL)
+    mm([(ap("MS", 16, 32), ap("BLKH"), ap("kh"), True, True)])
+    ts(ap("KR"), ap("MS", 16, 32), 2048.0, ADD)
+    ts(ap("th8h"), ap("th8"), -2048.0, ADD)
+    mm([(ap("MS", 8, 9), ap("REP8"), ap("th8h"), True, True)])
+    ts(ap("th16"), ap("MS", 8, 9), 2048.0, ADD, 256.0, MUL)
+    ts(ap("c8h"), ap("c8"), -2048.0, ADD)
+    mm([(ap("HR", 0, 256), ap("REP8"), ap("c8h"), True, True)])
+    act(ap("CX0", 0, 256), ap("HR", 0, 256), AF.Copy, bias=2048.0)
+    tt(ap("CM"), ap("CX0", 0, 256), ap("MWR"), MUL); scan(ap("CM2"), ap("RST"), ap("CM")); cp(ap("CL0"), ap("CM2", 15, 256, 16))
+    for k in "01":
+        fill(ap("TX" + k, 256, 640), 0.0)
+    act(ap("TX0", 0, 256), ind(ap("TP"), ap("CL0")), AF.Copy)
+    for s in range(16):
+        ts(ap("SEL", 128 * s, 128 * s + 128), ap("CSB"), float(s), EQ, 256.0, MUL)
+    ts(ap("k2I"), ap("CS", 0, 128), 7, AND); ts(ap("tmpA"), ap("k2I"), 1.0, ADD); tt(ap("tmpB"), ap("tmpA"), ap("BLKB"), MUL); ts(ap("C7B"), ap("tmpB"), -1.0, ADD)
+    for r in range(8):
+        ts(ap("SLP", 128 * r, 128 * r + 128), ap("C7B"), float(r), EQ, 256.0, MUL)
+    ts(ap("k2I"), ap("IC", 0, 128), 1, AND); ts(ap("s3F"), ap("sF"), 7.5, GT)
+    ts(ap("pz"), ap("k2I"), ap("s3F"), NE, 4194304.0, MUL)
+    ts(ap("t256", 0, 128), ap("IC", 0, 128), 5, SHR); ts(ap("tmpA"), ap("t256", 0, 128), 12.0, ADD, 16.0, MUL); tt(ap("MP"), ap("pz"), ap("tmpA"), ADD)
+    ts(ap("t256", 128, 256), ap("IC", 0, 128), 3, SHR); ts(ap("tmpA"), ap("t256", 128, 256), 16.0, MUL); tt(ap("ML"), ap("pz"), ap("tmpA"), ADD)
+    ts(ap("MC"), ap("CG"), 16.0, MUL)
+    ts(ap("CC"), ap("IC", 0, 16), 1.0, MUL); ts(ap("CCL"), ap("IC", 0, 4), 1.0, MUL)
+    ts(ap("JW0"), ap("IC", 0, 16), 16.0, MUL, ap("sF"), ADD)
+    ts(ap("J256"), ap("JW0"), 256.0, ADD); ts(ap("D4096"), ap("JW0"), 4096.0, ADD)
+    ts(ap("FIX", 0, 16), ap("JW0"), 254.5, GT, 256.0, MUL); ts(ap("FIX", 16, 32), ap("JW0"), 253.5, GT, 256.0, MUL)
+    ts(ap("CL"), ap("CC"), 16.0, MUL, 15.0, ADD)
+    ts(ap("oneR"), ap("CS"), -1.0, GT); ts(ap("EE", 0, 1), ap("pF"), 0.0, MUL)
+    ts(ap("tmpA"), ap("CS", 0, 128), ap("sF"), LE, -1.0, MUL); tt(ap("TRIMB"), ap("tmpA"), ap("BLKB"), MUL)
+    ts(ap("IDH"), ap("IC", 0, 128), ap("pF"), EQ); cp(ap("IDB"), ap("IDH")); ts(ap("IDN"), ap("IDH"), -1.0, MUL); ts(ap("EQM"), ap("MWR"), -1.0, ADD); fill(ap("ONEB"), 1.0); fill(ap("one16"), 1.0); fill(ap("C255"), 255.0)
+    ts(ap("TRP"), ap("CS"), ap("sF"), LE, 16384.0, MUL)
+    ts(ap("T5"), ap("IC"), 5.0, MUL, 2.0, ADD)
+    rng = []
+    for c in range(16):
+        lo = -((-(64 * c + 2)) // 5); hi = min(256, -((-(112 * c + 110)) // 5))
+        rng.append((lo, hi))
+    ts(ap("kz1"), ap("IC"), 5.0, MUL, 62.0, ADD); ts(ap("kz1"), ap("kz1"), 6, SHR); ts(ap("kz2"), ap("kz1"), 16.0, MIN)
+    ts(ap("kz1"), ap("T5"), -55.5, ADD, 1.0 / 112, MUL); tt(ap("KONST"), ap("kz2"), ap("kz1"), ADD)
+    fill(ap("RJ", 0, 16), 300.0)
+    ts(ap("IC64"), ap("IC", 0, 64), 1.0, MUL); ts(ap("PF64"), ap("IC64"), 5.0, MUL, 1280.0, ADD)
+    fill(ap("HT", 256, 768), UNF); fill(ap("lHT", 64, 128), UNF); fill(ap("RS", 128, 136), 0.0)
+
+    def sel(bank, o, name, lo, n):
+        return [(ap(bank, o, o + n), ap("SEL", 128 * s, 128 * s + 128), ap(name, lo + s, lo + s + 16 * (n - 1) + 1, 16), s == 0, s == 15) for s in range(16)]
+
+    for t in range(RO):
+        cur, nxt = str(t % 2), str(1 - t % 2)
+        cx, tx, cy, ty = "CX" + cur, "TX" + cur, "CX" + nxt, "TX" + nxt
+        last = t == RO - 1
+        b16 = ap("th16") if t == 0 else ap("b16a" if t % 2 else "b16b")
+        lst = []
+        for qv in (0, 1):
+            for r in range(4):
+                lst.append((ap("UVP", 64 * qv, 64 * qv + 64), wt(0, qv, r), ap(tx, r, r + 253, 4), r == 0, False))
+                lst.append((ap("UVP", 64 * qv, 64 * qv + 64), wt(1, qv, r), ap(tx, r + 1, r + 254, 4), False, r == 3))
+        mm(lst)
+        mm([(ap("ZP", 0, 256), ap("PL"), ap(tx, 0, 256), True, False), (ap("ZP", 0, 256), ap("PR"), ap(tx, 1, 257), False, True)])
+        act(ap("ZB"), ap("ZP", 0, 256), AF.Copy)
+        tt(ap("UVM"), ap("UVP", 0, 128), ap("MQ"), MUL)
+        tt(ap("UT"), ap("UVM", 0, 128, 2), ap("UVM", 1, 128, 2), ADD)
+        tt(ap("UVI"), ap("UT", 0, 64, 2), ap("UT", 1, 64, 2), ADD)
+        ts(ap("UVA"), ap("UVI"), 4095, AND)
+        tt(ap("UVW"), ap("UVA", 0, 16), ap("UVA", 16, 32), MUL)
+        ts(ap("UVA", 16, 32), ap("UVW"), 5, SHR)
+        cp(ap("UQ"), ap("UVA"))
+        for c in range(16):
+            if c % 4 == 3:
+                act(ap("HF", c // 4, 64, 4), ap("KR"), AF.Identity, bias=ap("UQ", 16 + c, 17 + c), scale=ap("UQ", c, c + 1))
+            else:
+                ts(ap("HV", c, 256, 16), ap("KR"), ap("UQ", c, c + 1), MUL, ap("UQ", 16 + c, 17 + c), ADD)
+        cp(ap("HV", 3, 256, 4), ap("HF"))
+        for h in (0, 1):
+            ts(ap("HI", 128 * h, 128 * h + 128), ap("HV", 128 * h, 128 * h + 128), 4095, AND)
+            cp(ap("HO", 128 * h, 128 * h + 128), ap("HI", 128 * h, 128 * h + 128))
+        for mb in range(4):
+            if mb == 1:
+                cp(ap("CI"), ap(cx, 0, 256)); ts(ap("CI3"), ap("CI"), 3, AND); ts(ap("W16"), ap("CI3"), 4.0, ADD)
+                scan(ap("EE", 256, 512), ap("oneR"), ap("W16")); later(mark); cp(ap("EE", 1, 256), ap("EE", 256, 511))
+                ee = len(ops) - 1
+                mm(sel("MS", 32, "EE", 0, 32))
+                ts(ap("FI"), ap("MS", 32, 64), 0.2 / 4096, MUL); ts(ap("EB"), ap("MS", 48, 64), -1.0 / 4096, MUL, 0.5, ADD)
+                ts(ap("FB"), ap("FI"), 256.0, MIN); tt(ap("FC"), ap("FB"), ap("FIX"), MAX)
+                tt(ap("NW"), ap("FC", 16, 32), ap("FC", 0, 16), SUB)
+                ts(ap("UN0"), ap("NW"), 0.0, EQ, 256.0, MUL); tt(ap("UNC"), ap("UN0"), ap("CC"), ADD)
+            for m in range(4 * mb, 4 * mb + 4):
+                x, u = ap("X", 256 * m, 256 * m + 256), ind(ap("US", 0, 4096), ap("HO", 16 * m, 16 * m + 16))
+                if m in BYS:
+                    act(x, u, AF.Copy)
+                else:
+                    tt(x, u, ap("ZB"), SUB)
+                if m == 1:
+                    mark = len(ops) - 1
+                if m == 5:
+                    later(ee)
+            for m, k in (((0, 2), (2, 1), (3, 1)), ((0, 2), (2, 2)), ((0, 2), (2, 2)), ((0, 1), (1, 1), (2, 1), (3, 1)))[mb]:
+                lo = 1024 * mb + 256 * m
+                if 4 * mb + m in BYS:
+                    bank = BYS[4 * mb + m]
+                    mm([(ap(bank, 256, 512), ap("IDB"), ap("X", lo, lo + 256), True, False), (ap(bank, 256, 512), ap("IDN"), ap("ZB"), False, True)])
+                    act(ap("A", lo, lo + 256), ap(bank, 256, 512), AF.Abs)
+                else:
+                    act(ap("A", lo, lo + 256 * k), ap("X", lo, lo + 256 * k), AF.Abs)
+            d = "DA" if mb % 2 == 0 else "DB"
+            if mb < 3:
+                mm([(ap(d, 0, 64), ap("SEL", 128 * s, 128 * s + 128), ap("A", 1024 * mb + s, 1024 * mb + s + 1009, 16), s == 0, s == 15) for s in range(16)])
+                tt(ap("K", 64 * mb, 64 * mb + 64), ap(d, 0, 64), ap("MC", 64 * mb, 64 * mb + 64), ADD)
+            if mb == 1:
+                tt(ap("K2"), ap("K", 0, 64), ap("K", 64, 128), MIN)
+            if mb == 2:
+                tt(ap("K3"), ap("K2"), ap("K", 128, 192), MIN); tt(ap("K5"), ap("K3", 0, 32), ap("K3", 32, 64), MIN)
+        for h in (0, 1):
+            d, lo = ("DB", "DA")[h], 3072 + 512 * h
+            mm([(ap(d, 128, 192), ap("SLP", 128 * r, 128 * r + 128), ap("A", lo + r, lo + 512, 8), r == 0, r == 7) for r in range(8)])
+            kp = ap("KP", 64 * h, 64 * h + 64)
+            tt(kp, ap(d, 128, 192), ap("MP", 64 * h, 64 * h + 64), ADD)
+            kq = ap("KQ", 32 * h, 32 * h + 32)
+            tt(kq, ap("KP", 64 * h, 64 * h + 63, 2), ap("KP", 64 * h + 1, 64 * h + 64, 2), MIN)
+            tt(ap("K6" if h == 0 else "K7"), ap("K5" if h == 0 else "K6"), kq, MIN)
+        ts(ap("HT", 0, 256), ap("HI"), -2047.0, ADD)
+        tt(ap("KEY"), ap("K7", 0, 16), ap("K7", 16, 32), MIN)
+        fill(ap("ZA", 0, 64), 1024.0)
+        ts(ap("PO"), ap("KEY"), b16, GE); tt(ap("PN"), ap("PO"), ap("NW"), MUL); scan(ap("SC"), ap("one16"), ap("PN"))
+        ts(ap("UA"), ap("PN"), 0.5, LT); tt(ap("PEN"), ap("UA"), ap("J256"), MUL)
+        pen = len(ops) - 1
+        mm([(ap("MS", 64, 80), ap("TRIMB"), ap("PN"), True, False), (ap("MS", 64, 80), ap("BLKB"), ap("SC"), False, False), (ap("MS", 64, 80), ap("IDH"), ap("PEN"), False, True)])
+        cp(ap("OF"), ap("MS", 64, 80))
+        cp(ind(ap("ZA"), ap("OF")), ap("ZB"))
+        lender = T.cores[(rank + 1 + t % 3) % 4]
+        borrower = T.cores[(rank - 1 - t % 3) % 4]
+
+        def send(o, a, sem, loc, dst):
+            rid, pid, se = topo.addr(dst)
+            m = 0
+            for e in topo.engines(core, dst)[:8]:
+                m |= 1 << e
+            put("G", lambda g: g.remote_dma(T[o][:, :], res(a), T.sem[sem], T.sem[loc], pid, rid, m), [a], [], 1.0, sem=loc, inc=0)
+            ops[-1]["n"] = len(topo.engines(core, dst)[:8])
+            put("N", None, [], [ap(o)], FLIGHT, sem=sem, inc=8)
+            ops[-1]["after"] = [len(ops) - 2]
+        send("ZL%d" % t, ap("ZA", 0, 64), "ask%d" % t, "la", lender)
+        if not last:
+            bn = "b16a" if t % 2 == 0 else "b16b"
+            mm([(ap("MS", 96, 97), ap("ONEB"), ap("SC", 15, 16), True, True)])
+            cp(ap("PPI"), ap("MS", 96, 97)); ts(ap("PPJ"), ap("PPI"), 63, AND); ts(ap(bn), ap("PPJ"), 256.0, MUL, ap("th16"), ADD)
+        cp(ap("KI"), ap("KEY")); later(pen); ts(ap("MI"), ap("KI"), 240, AND)
+        ts(ap("LA"), ap("PO"), 256.0, MUL); later(pen); tt(ap("LC"), ap("LA"), ap("UNC"), ADD); tt(ap("LD"), ap("LC"), ap("MI"), ADD); cp(ap("LL"), ap("LD"))
+        tt(ap("HM"), ind(ap("HT"), ap("LL")), ap("MWR"), MUL); later(pen)
+        scan(ap("HS"), ap("RST"), ap("HM"))
+        mm([(ap("HR", 0, 256), ap("BLKH"), ap("HM"), True, True)])
+        cp(ap("HRH"), ap("HR", 0, 256))
+        act(ap(cx, 256, 512), ap("HR", 0, 256), AF.Copy, bias=2047.0)
+        ts(ap("HW"), ap("HS", 15, 256, 16), 2047.0, ADD); tt(ap("HN"), ap("HW"), ap("D4096"), SUB); cp(ap("HL"), ap("HW"))
+        ts(ap("HG"), ap("HW"), 0.0, GE); tt(ap("HD"), ap("HG"), ap("HN"), MUL)
+        for c in range(15):
+            ts(ap("ET", 256 * c, 256 * c + 240 - 16 * c), ap("HRH", 16 * c + 16, 256), ap("HS", 16 * c + 15, 16 * c + 16), EQ)
+            mm([(ap("CT", 16 * c + 16, 256), ap("BLKB"), ap("ET", 256 * c, 256 * c + 240 - 16 * c), c == 0, False)])
+        et = len(ops) - 2
+        tt(ap("HRT"), ap("HR", 0, 256), ap("TRP"), ADD); later(et)
+        tt(ap("ET", 3840, 4096), ind(ap("HS"), ap("CL")), ap("HRT"), EQ)
+        mm([(ap("CT", 16, 256), ap("BLKB"), ap("ET", 3856, 4096), False, True), (ap("CT", 0, 16), ap("BLKB"), ap("ET", 3840, 3856), True, True)])
+        ctl = len(ops) - 1
+        ts(ap("UR"), ap("HRH"), UNF, EQ, -1.0, MUL)
+        tt(ap("WM"), ap("CT", 0, 256), ap("EQM"), EQ); scan(ap("WS"), ap("RST"), ap("WM"))
+        tt(ap("LO1"), ap("WS", 15, 256, 16), ap("HD"), MUL); tt(ap("LO2"), ap("LO1"), ap("D4096"), ADD); cp(ap("LO"), ap("LO2"))
+        cp(ind(ap("US"), ap("LO")), ap("C255"))
+        zl = "ZL%d" % t
+        lst = []
+        for qv in (0, 1):
+            for r in range(4):
+                lst.append((ap("UVP", 128 + 16 * qv, 144 + 16 * qv), wt(2, qv, r), ap(zl, r, r + 61, 4), r == 0, r == 3))
+        mm(lst)
+        luv = len(ops) - 1
+        for k in range(4):
+            act(ap("ZT", 64 * k, 64 * k + 64), ap(zl), AF.Copy)
+        tt(ap("lUVM"), ap("UVP", 128, 160), ap("MQ", 0, 32), MUL)
+        tt(ap("lUT"), ap("lUVM", 0, 32, 2), ap("lUVM", 1, 32, 2), ADD)
+        tt(ap("lUVI"), ap("lUT", 0, 16, 2), ap("lUT", 1, 16, 2), ADD)
+        ts(ap("lUVA"), ap("lUVI"), 4095, AND)
+        tt(ap("lUVW"), ap("lUVA", 0, 4), ap("lUVA", 4, 8), MUL)
+        ts(ap("lUVA", 4, 8), ap("lUVW"), 5, SHR)
+        cp(ap("lUQ"), ap("lUVA"))
+        for c in range(4):
+            ts(ap("lHV", c, 64, 4), ap("KR"), ap("lUQ", c, c + 1), MUL, ap("lUQ", 4 + c, 5 + c), ADD)
+        ts(ap("lHI"), ap("lHV"), 4095, AND); cp(ap("lHO"), ap("lHI")); ts(ap("lHT", 0, 64), ap("lHI"), -2047.0, ADD)
+        for mb in range(4):
+            x, u = ap("lX", 256 * mb, 256 * mb + 256), ind(ap("US", 0, 4096), ap("lHO", 16 * mb, 16 * mb + 16))
+            if mb == 3:
+                act(x, u, AF.Copy)
+            else:
+                tt(x, u, ap("ZT"), SUB)
+                lx = len(ops) - 1
+        mm([(ap("ZP", 256, 512), ap("IDB"), ap("lX", 768, 1024), True, False), (ap("ZP", 256, 512), ap("IDN"), ap("ZT"), False, True)])
+        for mb in range(3):
+            act(ap("lA", 256 * mb, 256 * mb + 256), ap("lX", 256 * mb, 256 * mb + 256), AF.Abs)
+        act(ap("lA", 768, 1024), ap("ZP", 256, 512), AF.Abs)
+        for h in (0, 1):
+            d = ("DB", "DA")[h]
+            mm([(ap(d, 64, 128), ap("SLP", 128 * r, 128 * r + 128), ap("lA", 512 * h + r, 512 * h + 512, 8), r == 0, r == 7) for r in range(8)])
+            tt(ap("lK", 64 * h, 64 * h + 64), ap(d, 64, 128), ap("ML", 64 * h, 64 * h + 64), ADD)
+        tt(ap("lK0"), ap("lK", 0, 64), ap("lK", 64, 128), MIN)
+        tt(ap("lK1"), ap("lK0", 0, 32), ap("lK0", 32, 64), MIN); tt(ap("lK2"), ap("lK1", 0, 16), ap("lK1", 16, 32), MIN)
+        tt(ap("lK3"), ap("lK2", 0, 8), ap("lK2", 8, 16), MIN); tt(ap("lKEY"), ap("lK3", 0, 7, 2), ap("lK3", 1, 8, 2), MIN)
+        ts(ap("lPO"), ap("lKEY"), b16, GE, 64.0, MUL); tt(ap("lLC"), ap("lPO"), ap("CCL"), ADD)
+        cp(ap("lKI"), ap("lKEY")); ts(ap("lMI"), ap("lKI"), 2, SHR, 60, AND)
+        tt(ap("lLD"), ap("lLC"), ap("lMI"), ADD); cp(ap("lLL"), ap("lLD"))
+        tt(ap("lHM"), ind(ap("lHT"), ap("lLL")), ap("MWR", 0, 64), MUL)
+        scan(ap("lHS"), ap("RST", 0, 64), ap("lHM"))
+        mm([(ap("HR", 256, 320), ap("BLKH"), ap("lHM"), True, True)])
+        cp(ap("lHRH"), ap("HR", 256, 320)); tt(ap("lHRT"), ap("HR", 256, 320), ap("TRP", 0, 64), ADD)
+        ts(ap("lHW"), ap("lHS", 15, 64, 16), 2047.0, ADD); tt(ap("lHD"), ap("lHW"), ap("D4096", 0, 4), SUB); cp(ap("lHL"), ap("lHW"))
+        ts(ap("lET", 256, 320), ap("lHRH"), UNF, EQ)
+        mm([(ap("CT", 256, 320), ap("BLKB"), ap("lET", 256, 320), True, False)])
+        for c in range(3):
+            ts(ap("lET", 64 * c, 64 * c + 48 - 16 * c), ap("lHRH", 16 * c + 16, 64), ap("lHS", 16 * c + 15, 16 * c + 16), EQ)
+            mm([(ap("CT", 272 + 16 * c, 320), ap("BLKB"), ap("lET", 64 * c, 64 * c + 48 - 16 * c), False, False)])
+        tt(ap("lET", 192, 256), ind(ap("lHS"), ap("CL", 0, 4)), ap("lHRT"), EQ)
+        mm([(ap("CT", 256, 320), ap("BLKB"), ap("lET", 192, 256), False, True)])
+        ts(ap("GR"), ap("CT", 256, 320), 0.0, EQ)
+        tt(ap("RS", 0, 64), ind(ap("TP"), ap("lHL")), ap("GR"), MUL)
+        tt(ap("RS", 64, 128), ind(ap("US", 0, 4096), ap("lHL")), ap("GR"), MUL)
+        tt(ap("GM"), ap("CT", 256, 320), ap("EQM", 0, 64), EQ); scan(ap("GS"), ap("RST", 0, 64), ap("GM"))
+        ts(ap("RS", 128, 132), ap("GS", 15, 64, 16), -256.0, MUL, 256.0, ADD)
+        send("RB%d" % t, ap("RS"), "rep%d" % t, "lr", borrower)
+        tt(ap("lO1"), ap("GS", 15, 64, 16), ap("lHD"), MUL); tt(ap("lO2"), ap("lO1"), ap("D4096", 0, 4), ADD); cp(ap("lLO"), ap("lO2"))
+        cp(ind(ap("US"), ap("lLO")), ap("C255", 0, 64))
+        lend = len(ops) - 1
+        mm([(ap("JP", 0, 256), ap("BLKB"), ap("KONST"), True, False)])
+        off = 0
+        for c in range(16):
+            lo, hi = rng[c]
+            act(ap("SG", off, off + hi - lo), ap("T5", lo, hi), AF.Sign, bias=ap("EB", c, c + 1))
+            mm([(ap("JP", lo, hi), ap("BLKB"), ap("SG", off, off + hi - lo), False, c == 15)])
+            off += (hi - lo + 15) // 16 * 16
+        act(ap("RJ", 1, 257), ap("JP", 0, 256), AF.Relu, bias=254.0, scale=-0.5)
+        mm(sel("JP", 256, "RJ", 1, 16)); later(ctl); later(luv)
+        ts(ap("JW"), ap("JP", 256, 272), -1.0 / 4096, MUL, 254.0, ADD); cp(ap("JL"), ap("JW"))
+        tt(ap("WN"), ap("CT", 0, 256), ap("UR"), EQ); later(lx)
+        tt(ap("FIRST"), ap("RJ", 1, 257), ap("RJ", 0, 256), NE); later(lx)
+        tt(ap("FW"), ind(ap("WN"), ap("JL")), ap("FIRST"), MUL); later(lx)
+        mm(sel("JP", 272, "FW", 0, 16))
+        ts(ap("LB"), ap("JP", 272, 288), 1.0 / 16, MUL); tt(ap("JX"), ap("LB"), ap("JW"), ADD); cp(ap("JL2"), ap("JX"))
+        if not last:
+            act(ap(tx, 256, 512), ind(ap("TP"), ap("HL")), AF.Copy)
+            act(ap(ty, 0, 256), ind(ap(tx, 0, 512), ap("JL2")), AF.Copy)
+        act(ap(cy, 0, 256), ind(ap(cx, 0, 512), ap("JL2")), AF.Copy)
+        act(ap("EA", 0, 64), ap("PF64"), AF.Copy)
+        cp(ind(ap("EA"), ap("OF")), ap("EE", 0, 256)); later(lend)
+        tt(ap("EM"), ap("EA", 0, 64), ap("MWR", 0, 64), MUL); scan(ap("EQ"), ap("RST", 0, 64), ap("EM"))
+        ts(ap("FAI"), ap("EQ", 15, 64, 16), 0.2, MUL); cp(ap("FA"), ap("FAI"))
+        rb = "RB%d" % t
+        tt(ap("OB"), ap(rb, 128, 132), ap("FA"), ADD); cp(ap("OBU"), ap("OB"))
+        if not last:
+            cp(ind(ap(ty), ap("OBU")), ap(rb, 0, 64))
+        ts(ind(ap(cy), ap("OBU")), ap("IC64"), 1.0, MUL, float(S + CAP * t), ADD)
+        dma(ext("yu", S + CAP * t, S + CAP * t + CAP), ap(rb, 64, 128), 2.0)
+        dma(ext("yc", L * t, L * t + L), ap(cy, 0, 256, 1, slice(0, 128, 16)), 2.0)
+    dma(ext("yu", 0, S), ap("US", 0, 4096), 6.0)
+    return ops
+
+
+def order(ops):
+    last = {}
+    for i, o in enumerate(ops):
+        pre = {}
+
+        def add(j, wait):
+            if j != i:
+                pre[j] = pre.get(j, False) or wait
+        for j in o.get("after", ()):
+            pre[j] = False
+        for kind in ("R", "W"):
+            for nm, lo, hi, st in o[kind]:
+                ps = nm in _PS
+                for j, k2, lo2, hi2, st2 in last.get(nm, []):
+                    same = ops[j]["q"] == o["q"]
+                    if ps:
+                        if same and o["q"] == "P":
+                            add(j, False)
+                        elif not same:
+                            add(j, True)
+                        continue
+                    if kind == "R" and k2 == "R":
+                        continue
+                    if hi <= lo2 or hi2 <= lo or (st == st2 and st > 1 and (lo - lo2) % st):
+                        continue
+                    add(j, True)
+        for kind in ("R", "W"):
+            for nm, lo, hi, st in o[kind]:
+                ps = nm in _PS
+                lst = last.setdefault(nm, [])
+                if ps:
+                    if lst and ops[lst[-1][0]]["q"] != o["q"]:
+                        keep = []
+                        other = [e for e in lst if ops[e[0]]["q"] != o["q"]]
+                        lst[:] = other[-40:]
+                elif kind == "W" and st == 1:
+                    lst[:] = [e for e in lst if not (lo <= e[2] and e[3] <= hi) or e[0] == i]
+                lst.append((i, kind, lo, hi, st))
+        o["pre"] = pre
+    n = len(ops)
+    succ = [[] for _ in range(n)]
+    for i, o in enumerate(ops):
+        for j in o["pre"]:
+            succ[j].append(i)
+    pri = [0.0] * n
+    for i in range(n - 1, -1, -1):
+        pri[i] = ops[i]["c"] + max([pri[k] + HOP for k in succ[i]], default=0.0)
+    left = [len(o["pre"]) for o in ops]
+    ready = {}
+    est = [0.0] * n
+    fin = [0.0] * n
+    free = {}
+    for i in range(n):
+        if left[i] == 0:
+            ready.setdefault(ops[i]["q"], []).append(i)
+    seq = []
+    while len(seq) < n:
+        best = None
+        for q, lst in ready.items():
+            if not lst:
+                continue
+            f = 0.0 if q == "N" else free.get(q, 0.0)
+            m = min(max(f, est[i]) for i in lst)
+            c = [i for i in lst if max(f, est[i]) <= m + 0.03]
+            b = max(c, key=lambda i: pri[i])
+            tm = max(f, est[b])
+            if best is None or tm < best[0]:
+                best = (tm, q, b)
+        tm, q, b = best
+        ready[q].remove(b)
+        o = ops[b]
+        o["t"] = tm
+        if q == "Y":
+            free[q] = tm + 0.1
+            fin[b] = tm + o["c"]
+        elif q == "N":
+            fin[b] = tm + o["c"]
+        else:
+            free[q] = tm + o["c"]
+            fin[b] = tm + o["c"]
+        seq.append(b)
+        for k in succ[b]:
+            left[k] -= 1
+            hop = (OWN if ops[k]["q"] == q else HOP) if ops[k]["pre"][b] else 0.0
+            est[k] = max(est[k], tm if ops[k]["q"] == q and not ops[k]["pre"][b] else fin[b] + hop)
+            if left[k] == 0:
+                ready.setdefault(ops[k]["q"], []).append(k)
+    return seq, max(fin)
+
+
+def rank_program(g, core, T, topo):
+    rank = T.rank_of(core)
+    if rank is None:
+        return
+    ops = build(rank, core, T, topo)
+    seq, _ = order(ops)
+    eng = {"V": g.vector, "S": g.scalar, "P": g.tensor, "G": g, "Y": g.sync}
+    total = {}
+    known = {q: {} for q in eng}
+    for i in seq:
+        o = ops[i]
+        q = o["q"]
+        if q == "N":
+            o["at"] = (o["sem"], o["inc"]); o["clock"] = {}
+            total[o["sem"]] = o["inc"]
+            continue
+        kn = known[q]
+        need = [ops[j] for j, w in o["pre"].items() if w]
+        need.sort(key=lambda p: -p.get("t", 0.0))
+        for p in need:
+            sem, val = p["at"]
+            if kn.get(sem, 0) >= val:
+                continue
+            eng[q].wait_ge(T.sem[sem], val)
+            kn[sem] = val
+            for a, b in p["clock"].items():
+                if kn.get(a, 0) < b:
+                    kn[a] = b
+        r = o["fn"](g)
+        if o["sem"] is None:
+            sem = "s" + q
+            total[sem] = total.get(sem, 0) + 1
+            r.then_inc(T.sem[sem], 1)
+        elif "n" in o:
+            sem = o["sem"]
+            total[sem] = total.get(sem, 0) + o["n"]
+        else:
+            sem = o["sem"]
+            total[sem] = o["inc"]
+            r.then_inc(T.sem[sem], o["inc"])
+        o["at"] = (sem, total[sem])
+        o["clock"] = dict(kn)
+    for sem, val in total.items():
+        g.wait_ge(T.sem[sem], val)

@@ -26,9 +26,10 @@ _b("WT", 24 * 128, H); _b("MQ", 128, F); _b("MC", 256, F); _b("MCL", 64, F); _b(
 _b("C255", 256, BF); _b("T5", 256, F); _b("KONST", 256, BF); _b("one16", 16, F); _b("oneR", 256, H); _b("CC", 16, F); _b("JW0", 16, F); _b("jI", 16, I)
 _b("J256", 16, F); _b("D4096", 16, F); _b("FIX", 32, F); _b("CLf", 16, F); _b("CL", 16, U16); _b("IC64", 64, F); _b("PF64", 64, F); _b("CCL", 4, F)
 for _k in "01":
-    _b("CX" + _k, 640, F); _b("TX" + _k, 640, BF)
+    _b("CX" + _k, 640, F); _b("TX" + _k, 640, BF); _b("WX" + _k, 640, BF)
+_b("WTAB", 4096, BF); _b("W64", 64, BF); _b("B256", 128, BF); _b("rsc", 1, F); _b("rs1", 1, F); _b("rs2", 1, F); _b("rs3", 1, F)
 _b("CM", 256, F); _b("CM2", 256, F); _b("CL0", 16, U16)
-_b("ZB", 256, BF); _b("UVM", 128, F); _b("UT", 64, F); _b("UVI", 32, I); _b("UVA", 32, I); _b("UVW", 16, I); _b("UQ", 32, F)
+_b("ZB", 512, BF); _b("UVM", 128, F); _b("UT", 64, F); _b("UVI", 32, I); _b("UVA", 32, I); _b("UVW", 16, I); _b("UQ", 32, F)
 _b("HV", 256, I); _b("HF", 64, F); _b("HI", 256, I); _b("HO", 256, U16); _b("HT", 768, F)
 _b("X", 4096, BF); _b("A", 4096, BF); _b("K", 256, F); _b("K2", 64, F); _b("K3", 64, F); _b("K5", 32, F); _b("K6", 32, F); _b("K7", 32, F); _b("KP", 128, F); _b("KQ", 64, F); _b("MP", 128, F); _b("ML", 128, F); _b("SLP", 1024, BF); _b("s3F", 1, F); _b("k2I", 128, I); _b("pz", 128, F); _b("kz1", 256, I); _b("kz2", 256, F); _b("C7B", 128, BF); _b("HN", 16, F); _b("HG", 16, F); _b("UR", 256, BF); _b("KEY", 16, F)
 _b("PO", 16, F); _b("PN", 16, BF); _b("SC", 16, BF); _b("UA", 16, F); _b("PEN", 16, H); _b("OF", 16, U16); _b("ZA", 768, BF)
@@ -40,21 +41,21 @@ _b("CI", 256, I); _b("CI3", 256, I); _b("W16", 256, H); _b("EE", 512, H); _b("FI
 _b("EB", 16, F); _b("SG", 4096, BF); _b("RJ", 272, BF); _b("FIRST", 256, BF); _b("JW", 16, F); _b("JL", 16, U16); _b("FW", 256, BF); _b("JX", 16, F); _b("JL2", 16, U16)
 _b("EA", 768, F); _b("EM", 64, F); _b("EQ", 64, F); _b("FAI", 4, I); _b("FA", 4, F); _b("OB", 4, F); _b("OBU", 4, U16)
 for _k in range(RO):
-    _b("ZL%d" % _k, 64, BF); _b("RB%d" % _k, 136, BF)
+    _b("ZL%d" % _k, 64, BF); _b("RB%d" % _k, 72, BF); _b("RV%d" % _k, 64, BF)
 _b("ZT", 256, BF); _b("lUVM", 32, F); _b("lUT", 16, F); _b("lUVI", 8, I); _b("lUVA", 8, I); _b("lUVW", 4, I); _b("lUQ", 8, F)
 _b("lHV", 64, I); _b("lHI", 64, I); _b("lHO", 64, U16); _b("lHT", 128, F); _b("lX", 1024, BF); _b("lA", 1024, BF)
 _b("lK", 128, F); _b("lK0", 64, F); _b("lK1", 32, F); _b("lK2", 16, F); _b("lK3", 8, F); _b("lKEY", 4, F); _b("lKI", 4, I); _b("lMI", 4, I); _b("lPO", 4, F); _b("lLA", 4, F); _b("lLB", 4, F)
 _b("lLC", 4, F); _b("lLD", 4, F); _b("lLL", 4, U16); _b("lHM", 64, H); _b("lHS", 64, F); _b("lHRH", 64, H); _b("lHRT", 64, F); _b("lHW", 4, F); _b("lHD", 4, F); _b("lHL", 4, U16)
-_b("lET", 320, BF); _b("GR", 64, BF); _b("GM", 64, F); _b("GS", 64, F); _b("RS", 136, BF); _b("lO1", 4, F); _b("lO2", 4, F); _b("lLO", 4, U16)
+_b("lET", 320, BF); _b("GR", 64, BF); _b("GM", 64, F); _b("GS", 64, F); _b("RS", 72, BF); _b("RSU", 64, BF); _b("lO1", 4, F); _b("lO2", 4, F); _b("lLO", 4, U16)
 _PS = ["UVP", "ZP", "DA", "DB", "HR", "CT", "MS", "JP"]
 _SIZE = {F: 4, BF: 2, H: 2, I: 4, U16: 2}
 _OWN = ("US", "TP", "X", "A", "ZA")
-BYS = {3: "ZP", 12: "CT", 13: "ZP"}
+BYS = {12: "CT", 13: "ZP"}
 SCRATCH = {}
 _AT = {}
 _fill = {}
 for _n, (_w, _sh, _d) in _B.items():
-    if _n in _OWN or _n[:2] in ("ZL", "RB", "RS") or _sh[0] != 128:
+    if _n in _OWN or _n[:2] in ("ZL", "RB", "RV") or _n in ("RS", "RSU") or _sh[0] != 128:
         SCRATCH[_n] = (_w, _sh, _d); _AT[_n] = (_n, 0)
     else:
         _q = 32 // _SIZE[_d]
@@ -65,7 +66,7 @@ for _d, _c in _fill.items():
 for _n in _PS:
     SCRATCH[_n] = ("psum", [128, 512], F); _AT[_n] = (_n, 0); _B[_n] = SCRATCH[_n]
 ND = 24
-SEMAPHORES = ["sV", "sS", "sP", "sG", "la", "lr"] + ["ask%d" % k for k in range(RO)] + ["rep%d" % k for k in range(RO)] + ["d%d" % k for k in range(ND)]
+SEMAPHORES = ["sV", "sS", "sP", "sG", "la", "lr", "lu"] + ["reu%d" % k for k in range(RO)] + ["ask%d" % k for k in range(RO)] + ["rep%d" % k for k in range(RO)] + ["d%d" % k for k in range(ND)]
 
 CY = 0.001
 GA, SCT = 1.56, 3.8
@@ -217,10 +218,17 @@ def build(rank, core, T, topo):
     def wt(k, qv, r):
         i = (k * 2 + qv) * 4 + r
         return ap("WT", i * 128, i * 128 + 128)
-    for k, nm in enumerate(("wl", "wr", "hwg")):
-        for qv in (0, 1):
-            for r in range(4):
-                ts(wt(k, qv, r), ap("CQB"), float(r), EQ, ap(nm, qv, qv + 1), MUL)
+    ts(ap("rsc"), ap("slt8"), -1.0, MUL)
+    for r in (1, 2, 3):
+        ts(ap("rs%d" % r), ap("rsc"), float(r), ADD)
+    for qv in (0, 1):
+        ts(wt(0, qv, 0), ap("CQB"), 0.0, EQ, ap("wl", qv, qv + 1), MUL)
+        for r in (1, 2, 3):
+            ts(wt(0, qv, r), ap("CQB"), ap("rs%d" % r), EQ, ap("ws", qv, qv + 1), MUL)
+        ts(wt(1, qv, 3), ap("CQB"), 3.0, EQ, ap("wr", qv, qv + 1), MUL)
+    for qv in (0, 1):
+        for r in range(4):
+            ts(wt(2, qv, r), ap("CQB"), float(r), EQ, ap("hwg", qv, qv + 1), MUL)
     ts(ap("MQ"), ap("C3"), ap("s2F"), EQ)
     ts(ap("MWR"), ap("CS"), ap("sF"), EQ); ts(ap("RST"), ap("CS"), 0.5, GT)
     ts(ap("ksc"), ap("kmi"), -2048.0, ADD); ts(ap("kh"), ap("CS", 0, 16), ap("sF"), EQ, ap("ksc"), MUL)
@@ -236,11 +244,17 @@ def build(rank, core, T, topo):
     for k in "01":
         fill(ap("TX" + k, 256, 640), 0.0)
     act(ap("TX0", 0, 256), ind(ap("TP"), ap("CL0")), AF.Copy)
+    ts(ap("B256"), ap("BLKB"), 256.0, MUL)
+
+    def keep(o, pattern, base):
+        put("G", lambda g: g.affine_select(res(o), res(ap("B256")), pattern, EQ, 0.0, base, 0), [ap("B256")], [o], 0.4)
     for s in range(16):
-        ts(ap("SEL", 128 * s, 128 * s + 128), ap("CSB"), float(s), EQ, 256.0, MUL)
-    ts(ap("k2I"), ap("CS", 0, 128), 7, AND); ts(ap("tmpA"), ap("k2I"), 1.0, ADD); tt(ap("tmpB"), ap("tmpA"), ap("BLKB"), MUL); ts(ap("C7B"), ap("tmpB"), -1.0, ADD)
+        keep(ap("SEL", 128 * s, 128 * s + 128), [[0, 8], [1, 16]], -s)
     for r in range(8):
-        ts(ap("SLP", 128 * r, 128 * r + 128), ap("C7B"), float(r), EQ, 256.0, MUL)
+        keep(ap("SLP", 128 * r, 128 * r + 128), [[0, 16], [1, 8]], -r)
+    put("G", lambda g: g.iota(res(ap("WTAB")), [[0, 1024], [1, 4]], 4, 0, allow_small_or_imprecise_dtypes=True), [], [ap("WTAB")], 7.0)
+    cp(ap("CI"), ap("CX0", 0, 256)); ts(ap("CI3"), ap("CI"), 3, AND); ts(ap("WX0", 0, 256), ap("CI3"), 4.0, ADD)
+    ts(ap("W64"), ap("C3", 0, 64), 4.0, ADD)
     ts(ap("k2I"), ap("IC", 0, 128), 1, AND); ts(ap("s3F"), ap("sF"), 7.5, GT)
     ts(ap("pz"), ap("k2I"), ap("s3F"), NE, 4194304.0, MUL)
     ts(ap("t256", 0, 128), ap("IC", 0, 128), 5, SHR); ts(ap("tmpA"), ap("t256", 0, 128), 12.0, ADD, 16.0, MUL); tt(ap("MP"), ap("pz"), ap("tmpA"), ADD)
@@ -264,24 +278,24 @@ def build(rank, core, T, topo):
     ts(ap("kz1"), ap("T5"), -55.5, ADD, 1.0 / 112, MUL); tt(ap("KONST"), ap("kz2"), ap("kz1"), ADD)
     fill(ap("RJ", 0, 16), 300.0)
     ts(ap("IC64"), ap("IC", 0, 64), 1.0, MUL); ts(ap("PF64"), ap("IC64"), 5.0, MUL, 1280.0, ADD)
-    fill(ap("HT", 256, 768), UNF); fill(ap("lHT", 64, 128), UNF); fill(ap("RS", 128, 136), 0.0)
+    fill(ap("HT", 256, 768), UNF); fill(ap("lHT", 64, 128), UNF); fill(ap("RS", 64, 72), 0.0)
 
     def sel(bank, o, name, lo, n):
         return [(ap(bank, o, o + n), ap("SEL", 128 * s, 128 * s + 128), ap(name, lo + s, lo + s + 16 * (n - 1) + 1, 16), s == 0, s == 15) for s in range(16)]
 
     for t in range(RO):
         cur, nxt = str(t % 2), str(1 - t % 2)
-        cx, tx, cy, ty = "CX" + cur, "TX" + cur, "CX" + nxt, "TX" + nxt
+        cx, tx, cy, ty, wx, wy = "CX" + cur, "TX" + cur, "CX" + nxt, "TX" + nxt, "WX" + cur, "WX" + nxt
         last = t == RO - 1
         b16 = ap("th16") if t == 0 else ap("b16a" if t % 2 else "b16b")
         lst = []
         for qv in (0, 1):
             for r in range(4):
                 lst.append((ap("UVP", 64 * qv, 64 * qv + 64), wt(0, qv, r), ap(tx, r, r + 253, 4), r == 0, False))
-                lst.append((ap("UVP", 64 * qv, 64 * qv + 64), wt(1, qv, r), ap(tx, r + 1, r + 254, 4), False, r == 3))
+            lst.append((ap("UVP", 64 * qv, 64 * qv + 64), wt(1, qv, 3), ap(tx, 4, 257, 4), False, True))
         mm(lst)
         mm([(ap("ZP", 0, 256), ap("PL"), ap(tx, 0, 256), True, False), (ap("ZP", 0, 256), ap("PR"), ap(tx, 1, 257), False, True)])
-        act(ap("ZB"), ap("ZP", 0, 256), AF.Copy)
+        act(ap("ZB", 0, 256), ap("ZP", 0, 256), AF.Copy); act(ap("ZB", 256, 512), ap("ZP", 0, 256), AF.Copy)
         tt(ap("UVM"), ap("UVP", 0, 128), ap("MQ"), MUL)
         tt(ap("UT"), ap("UVM", 0, 128, 2), ap("UVM", 1, 128, 2), ADD)
         tt(ap("UVI"), ap("UT", 0, 64, 2), ap("UT", 1, 64, 2), ADD)
@@ -299,10 +313,8 @@ def build(rank, core, T, topo):
             ts(ap("HI", 128 * h, 128 * h + 128), ap("HV", 128 * h, 128 * h + 128), 4095, AND)
             cp(ap("HO", 128 * h, 128 * h + 128), ap("HI", 128 * h, 128 * h + 128))
         for mb in range(4):
-            if mb == 1:
-                cp(ap("CI"), ap(cx, 0, 256)); ts(ap("CI3"), ap("CI"), 3, AND); ts(ap("W16"), ap("CI3"), 4.0, ADD)
-                scan(ap("EE", 256, 512), ap("oneR"), ap("W16")); later(mark); cp(ap("EE", 1, 256), ap("EE", 256, 511))
-                ee = len(ops) - 1
+            if mb == 0:
+                scan(ap("EE", 256, 512), ap("oneR"), ap(wx, 0, 256)); cp(ap("EE", 1, 256), ap("EE", 256, 511))
                 mm(sel("MS", 32, "EE", 0, 32))
                 ts(ap("FI"), ap("MS", 32, 64), 0.2 / 4096, MUL); ts(ap("EB"), ap("MS", 48, 64), -1.0 / 4096, MUL, 0.5, ADD)
                 ts(ap("FB"), ap("FI"), 256.0, MIN); tt(ap("FC"), ap("FB"), ap("FIX"), MAX)
@@ -312,20 +324,22 @@ def build(rank, core, T, topo):
                 x, u = ap("X", 256 * m, 256 * m + 256), ind(ap("US", 0, 4096), ap("HO", 16 * m, 16 * m + 16))
                 if m in BYS:
                     act(x, u, AF.Copy)
-                else:
-                    tt(x, u, ap("ZB"), SUB)
-                if m == 1:
-                    mark = len(ops) - 1
-                if m == 5:
-                    later(ee)
-            for m, k in (((0, 2), (2, 1), (3, 1)), ((0, 2), (2, 2)), ((0, 2), (2, 2)), ((0, 1), (1, 1), (2, 1), (3, 1)))[mb]:
+                elif m in (14, 15):
+                    tt(x, u, ap("ZB", 0, 256), SUB)
+                elif m % 2 == 0:
+                    tt(ap("X", 256 * m, 256 * m + 512), ind(ap("US", 0, 4096), ap("HO", 16 * m, 16 * m + 32)), ap("ZB"), SUB)
+            for m, k in (((0, 2), (2, 2)), ((0, 2), (2, 2)), ((0, 2), (2, 2)), ((0, 1), (1, 1), (2, 1), (3, 1)))[mb]:
                 lo = 1024 * mb + 256 * m
                 if 4 * mb + m in BYS:
                     bank = BYS[4 * mb + m]
-                    mm([(ap(bank, 256, 512), ap("IDB"), ap("X", lo, lo + 256), True, False), (ap(bank, 256, 512), ap("IDN"), ap("ZB"), False, True)])
+                    mm([(ap(bank, 256, 512), ap("IDB"), ap("X", lo, lo + 256), True, False), (ap(bank, 256, 512), ap("IDN"), ap("ZB", 0, 256), False, True)])
                     act(ap("A", lo, lo + 256), ap(bank, 256, 512), AF.Abs)
+                    if mb == 3:
+                        later(third)
                 else:
                     act(ap("A", lo, lo + 256 * k), ap("X", lo, lo + 256 * k), AF.Abs)
+                    if mb == 2:
+                        third = len(ops) - 1
             d = "DA" if mb % 2 == 0 else "DB"
             if mb < 3:
                 mm([(ap(d, 0, 64), ap("SEL", 128 * s, 128 * s + 128), ap("A", 1024 * mb + s, 1024 * mb + s + 1009, 16), s == 0, s == 15) for s in range(16)])
@@ -350,7 +364,7 @@ def build(rank, core, T, topo):
         pen = len(ops) - 1
         mm([(ap("MS", 64, 80), ap("TRIMB"), ap("PN"), True, False), (ap("MS", 64, 80), ap("BLKB"), ap("SC"), False, False), (ap("MS", 64, 80), ap("IDH"), ap("PEN"), False, True)])
         cp(ap("OF"), ap("MS", 64, 80))
-        cp(ind(ap("ZA"), ap("OF")), ap("ZB"))
+        cp(ind(ap("ZA"), ap("OF")), ap("ZB", 0, 256))
         lender = T.cores[(rank + 1 + t % 3) % 4]
         borrower = T.cores[(rank - 1 - t % 3) % 4]
 
@@ -443,10 +457,11 @@ def build(rank, core, T, topo):
         mm([(ap("CT", 256, 320), ap("BLKB"), ap("lET", 192, 256), False, True)])
         ts(ap("GR"), ap("CT", 256, 320), 0.0, EQ)
         tt(ap("RS", 0, 64), ind(ap("TP"), ap("lHL")), ap("GR"), MUL)
-        tt(ap("RS", 64, 128), ind(ap("US", 0, 4096), ap("lHL")), ap("GR"), MUL)
         tt(ap("GM"), ap("CT", 256, 320), ap("EQM", 0, 64), EQ); scan(ap("GS"), ap("RST", 0, 64), ap("GM"))
-        ts(ap("RS", 128, 132), ap("GS", 15, 64, 16), -256.0, MUL, 256.0, ADD)
+        ts(ap("RS", 64, 68), ap("GS", 15, 64, 16), -256.0, MUL, 256.0, ADD)
         send("RB%d" % t, ap("RS"), "rep%d" % t, "lr", borrower)
+        tt(ap("RSU"), ind(ap("US", 0, 4096), ap("lHL")), ap("GR"), MUL)
+        send("RV%d" % t, ap("RSU"), "reu%d" % t, "lu", borrower)
         tt(ap("lO1"), ap("GS", 15, 64, 16), ap("lHD"), MUL); tt(ap("lO2"), ap("lO1"), ap("D4096", 0, 4), ADD); cp(ap("lLO"), ap("lO2"))
         cp(ind(ap("US"), ap("lLO")), ap("C255", 0, 64))
         lend = len(ops) - 1
@@ -467,18 +482,20 @@ def build(rank, core, T, topo):
         ts(ap("LB"), ap("JP", 272, 288), 1.0 / 16, MUL); tt(ap("JX"), ap("LB"), ap("JW"), ADD); cp(ap("JL2"), ap("JX"))
         if not last:
             act(ap(tx, 256, 512), ind(ap("TP"), ap("HL")), AF.Copy)
+            act(ap(wx, 256, 512), ind(ap("WTAB"), ap("HL")), AF.Copy)
             act(ap(ty, 0, 256), ind(ap(tx, 0, 512), ap("JL2")), AF.Copy)
+            act(ap(wy, 0, 256), ind(ap(wx, 0, 512), ap("JL2")), AF.Copy)
         act(ap(cy, 0, 256), ind(ap(cx, 0, 512), ap("JL2")), AF.Copy)
         act(ap("EA", 0, 64), ap("PF64"), AF.Copy)
         cp(ind(ap("EA"), ap("OF")), ap("EE", 0, 256)); later(lend)
         tt(ap("EM"), ap("EA", 0, 64), ap("MWR", 0, 64), MUL); scan(ap("EQ"), ap("RST", 0, 64), ap("EM"))
         ts(ap("FAI"), ap("EQ", 15, 64, 16), 0.2, MUL); cp(ap("FA"), ap("FAI"))
         rb = "RB%d" % t
-        tt(ap("OB"), ap(rb, 128, 132), ap("FA"), ADD); cp(ap("OBU"), ap("OB"))
+        tt(ap("OB"), ap(rb, 64, 68), ap("FA"), ADD); cp(ap("OBU"), ap("OB"))
         if not last:
-            cp(ind(ap(ty), ap("OBU")), ap(rb, 0, 64))
+            cp(ind(ap(ty), ap("OBU")), ap(rb, 0, 64)); cp(ind(ap(wy), ap("OBU")), ap("W64"))
         ts(ind(ap(cy), ap("OBU")), ap("IC64"), 1.0, MUL, float(S + CAP * t), ADD)
-        dma(ext("yu", S + CAP * t, S + CAP * t + CAP), ap(rb, 64, 128), 2.0)
+        dma(ext("yu", S + CAP * t, S + CAP * t + CAP), ap("RV%d" % t), 2.0)
         dma(ext("yc", L * t, L * t + L), ap(cy, 0, 256, 1, slice(0, 128, 16)), 2.0)
     dma(ext("yu", 0, S), ap("US", 0, 4096), 6.0)
     return ops

@@ -30,8 +30,8 @@ for _k in "01":
 _b("WTAB", 4096, BF); _b("W64", 64, BF); _b("B256", 128, BF); _b("rsc", 1, F); _b("rs1", 1, F); _b("rs2", 1, F); _b("rs3", 1, F)
 _b("CM", 256, F); _b("CM2", 256, F); _b("CL0", 16, U16)
 _b("ZB", 512, BF); _b("UVM", 128, F); _b("UT", 64, F); _b("UVI", 32, I); _b("UVA", 32, I); _b("UVW", 16, I); _b("UQ", 32, F)
-_b("HV", 256, I); _b("HF", 64, F); _b("HI", 256, I); _b("HO", 256, U16); _b("HT", 768, F)
-_b("X", 4096, BF); _b("A", 4096, BF); _b("K", 256, F); _b("K2", 64, F); _b("K3", 64, F); _b("K5", 32, F); _b("K6", 32, F); _b("K7", 32, F); _b("KP", 128, F); _b("KQ", 64, F); _b("MP", 128, F); _b("ML", 128, F); _b("SLP", 1024, BF); _b("s3F", 1, F); _b("k2I", 128, I); _b("pz", 128, F); _b("kz1", 256, I); _b("kz2", 256, F); _b("C7B", 128, BF); _b("HN", 16, F); _b("HG", 16, F); _b("UR", 256, BF); _b("KEY", 16, F)
+_b("HV", 256, I); _b("HF", 64, F); _b("HI", 256, I); _b("HO", 256, U16); _b("HT", 1056, F)
+_b("X", 4096, BF); _b("A", 4096, BF); _b("K", 256, F); _b("K2", 64, F); _b("K3", 64, F); _b("K5", 32, F); _b("RM", 576, F); _b("KQ", 32, F); _b("MP", 512, BF); _b("k3I", 64, I); _b("PZ", 64, BF); _b("PZQ", 64, BF); _b("SLQ", 512, BF); _b("B512", 128, BF); _b("lRM", 320, F); _b("ML", 256, BF); _b("SLP", 1024, BF); _b("s3F", 1, F); _b("k2I", 128, I); _b("pz", 128, F); _b("kz1", 256, I); _b("kz2", 256, F); _b("C7B", 128, BF); _b("TRH", 256, H); _b("BLK8", 128, BF); _b("ID8", 128, BF); _b("NM", 256, BF); _b("RSTB", 256, F); _b("WD", 256, BF); _b("UR", 256, BF); _b("KEY", 16, I)
 _b("PO", 16, F); _b("PN", 16, BF); _b("SC", 16, BF); _b("UA", 16, F); _b("PEN", 16, H); _b("OF", 16, U16); _b("ZA", 768, BF)
 _b("PPI", 1, I); _b("PPJ", 1, I); _b("PPF", 1, F)
 _b("KI", 16, I); _b("MI", 16, I); _b("LA", 16, F); _b("LB", 16, F); _b("LC", 16, F); _b("LD", 16, F); _b("LL", 16, U16)
@@ -43,14 +43,17 @@ _b("EA", 768, F); _b("EM", 64, F); _b("EQ", 64, F); _b("FAI", 4, I); _b("FA", 4,
 for _k in range(RO):
     _b("ZL%d" % _k, 64, BF); _b("RB%d" % _k, 72, BF); _b("RV%d" % _k, 64, BF)
 _b("ZT", 256, BF); _b("lUVM", 32, F); _b("lUT", 16, F); _b("lUVI", 8, I); _b("lUVA", 8, I); _b("lUVW", 4, I); _b("lUQ", 8, F)
-_b("lHV", 64, I); _b("lHI", 64, I); _b("lHO", 64, U16); _b("lHT", 128, F); _b("lX", 1024, BF); _b("lA", 1024, BF)
-_b("lK", 128, F); _b("lK0", 64, F); _b("lK1", 32, F); _b("lK2", 16, F); _b("lK3", 8, F); _b("lKEY", 4, F); _b("lKI", 4, I); _b("lMI", 4, I); _b("lPO", 4, F); _b("lLA", 4, F); _b("lLB", 4, F)
+_b("lHV", 64, I); _b("lHI", 64, I); _b("lHO", 64, U16); _b("lHT", 144, F); _b("lX", 1024, BF); _b("lA", 1024, BF)
+_b("lK", 128, F); _b("lK0", 64, F); _b("lK1", 32, F); _b("lK2", 16, F); _b("lK3", 8, F); _b("lKEY", 4, I); _b("lKI", 4, I); _b("lMI", 4, I); _b("lPO", 4, F); _b("lLA", 4, F); _b("lLB", 4, F)
 _b("lLC", 4, F); _b("lLD", 4, F); _b("lLL", 4, U16); _b("lHM", 64, H); _b("lHS", 64, F); _b("lHRH", 64, H); _b("lHRT", 64, F); _b("lHW", 4, F); _b("lHD", 4, F); _b("lHL", 4, U16)
 _b("lET", 320, BF); _b("GR", 64, BF); _b("GM", 64, F); _b("GS", 64, F); _b("RS", 72, BF); _b("RSU", 64, BF); _b("lO1", 4, F); _b("lO2", 4, F); _b("lLO", 4, U16)
 _PS = ["UVP", "ZP", "DA", "DB", "HR", "CT", "MS", "JP"]
 _SIZE = {F: 4, BF: 2, H: 2, I: 4, U16: 2}
 _OWN = ("US", "TP", "X", "A", "ZA")
-BYS = {12: "CT", 13: "ZP"}
+NET = 0
+XCH = False
+HB = (0, 1, 2, 3, 4, 6, 5, 7)
+BYS = {3: "ZP", 7: "CT", 13: "ZP"}
 SCRATCH = {}
 _AT = {}
 _fill = {}
@@ -71,11 +74,13 @@ SEMAPHORES = ["sV", "sS", "sP", "sG", "la", "lr", "lu"] + ["reu%d" % k for k in 
 CY = 0.001
 GA, SCT = 1.56, 3.8
 HOP, OWN = 0.10, 0.05
-FLIGHT = 2.6
+FLIGHT = 2.8
+AHEAD = 0.0
 
 
 def build(rank, core, T, topo):
     ops = []
+    start = [-1000]
 
     def ap(name, lo=0, hi=None, st=1, rows=None):
         hi = _B[name][1][1] if hi is None else hi
@@ -123,7 +128,7 @@ def build(rank, core, T, topo):
                 W += acc(d[1]); R += acc(d[2])
             else:
                 W += acc(d)
-        ops.append({"q": q, "fn": fn, "R": R, "W": W, "c": cost, "sem": sem, "inc": inc})
+        ops.append({"q": q, "fn": fn, "R": R, "W": W, "c": cost, "sem": sem, "inc": inc, "k": len(ops) - start[0]})
 
     class V:
         pass
@@ -156,8 +161,8 @@ def build(rank, core, T, topo):
         two = 0.5 if a[0] == "a" and o[0] == "a" and not isps(a) and size(a) == 2 and size(o) == 2 else 1
         put("V", lambda g: g.vector.tensor_copy(res(o), res(a)), [a], [o], vcost(n_of(o), two, a[0] == "i", o[0] == "i"))
 
-    def scan(o, a, b):
-        put("V", lambda g: g.vector.tensor_tensor_scan(res(o), res(a), res(b), 0.0, MUL, ADD), [a, b], [o], vcost(n_of(o), 1, False, False))
+    def scan(o, a, b, op0=AluOpType.mult, op1=AluOpType.add):
+        put("V", lambda g: g.vector.tensor_tensor_scan(res(o), res(a), res(b), 0.0, op0, op1), [a, b], [o], vcost(n_of(o), 1, False, False))
 
     def fill(o, v):
         put("V", lambda g: g.vector.memset(res(o), v), [], [o], vcost(n_of(o), 0.5, False, False))
@@ -236,7 +241,7 @@ def build(rank, core, T, topo):
     ts(ap("KR"), ap("MS", 16, 32), 2048.0, ADD)
     ts(ap("th8h"), ap("th8"), -2048.0, ADD)
     mm([(ap("MS", 8, 9), ap("REP8"), ap("th8h"), True, True)])
-    ts(ap("th16"), ap("MS", 8, 9), 2048.0, ADD, 256.0, MUL)
+    ts(ap("th16"), ap("MS", 8, 9), 2048.0 - 1.0 / 512, ADD, 512.0, MUL)
     ts(ap("c8h"), ap("c8"), -2048.0, ADD)
     mm([(ap("HR", 0, 256), ap("REP8"), ap("c8h"), True, True)])
     act(ap("CX0", 0, 256), ap("HR", 0, 256), AF.Copy, bias=2048.0)
@@ -244,22 +249,30 @@ def build(rank, core, T, topo):
     for k in "01":
         fill(ap("TX" + k, 256, 640), 0.0)
     act(ap("TX0", 0, 256), ind(ap("TP"), ap("CL0")), AF.Copy)
-    ts(ap("B256"), ap("BLKB"), 256.0, MUL)
+    act(ap("BLK8"), ap("BLKB"), AF.Copy, scale=8192.0);
+    ts(ap("NM"), ap("CS"), ap("sF"), NE, 4194304.0, MUL); ts(ap("RSTB"), ap("CS"), 0.5, LT, 8388608.0, MUL)
+    act(ap("B512"), ap("BLKB"), AF.Copy, scale=512.0); act(ap("B256"), ap("BLKB"), AF.Copy, scale=16.0)
 
-    def keep(o, pattern, base):
-        put("G", lambda g: g.affine_select(res(o), res(ap("B256")), pattern, EQ, 0.0, base, 0), [ap("B256")], [o], 0.4)
-    for s in range(16):
-        keep(ap("SEL", 128 * s, 128 * s + 128), [[0, 8], [1, 16]], -s)
+
+    def keep(o, src, pattern, base):
+        put("G", lambda g: g.affine_select(res(o), res(ap(src)), pattern, EQ, 0.0, base, 0), [ap(src)], [o], 0.4)
     for r in range(8):
-        keep(ap("SLP", 128 * r, 128 * r + 128), [[0, 16], [1, 8]], -r)
-    put("G", lambda g: g.iota(res(ap("WTAB")), [[0, 1024], [1, 4]], 4, 0, allow_small_or_imprecise_dtypes=True), [], [ap("WTAB")], 7.0)
+        keep(ap("SLP", 128 * r, 128 * r + 128), "B512", [[0, 16], [1, 8]], -r)
+    slp = len(ops) - 1
+    for s in range(16):
+        keep(ap("SEL", 128 * s, 128 * s + 128), "B256", [[0, 8], [1, 16]], -s); later(slp)
+    slp = len(ops) - 1
+    for r in range(4):
+        keep(ap("SLQ", 128 * r, 128 * r + 128), "B512", [[0, 32], [1, 4]], -r); later(slp)
+    slp = len(ops) - 1
+    put("G", lambda g: g.iota(res(ap("WTAB")), [[0, 1024], [1, 4]], 4, 0, allow_small_or_imprecise_dtypes=True), [], [ap("WTAB")], 7.0); later(slp)
     cp(ap("CI"), ap("CX0", 0, 256)); ts(ap("CI3"), ap("CI"), 3, AND); ts(ap("WX0", 0, 256), ap("CI3"), 4.0, ADD)
     ts(ap("W64"), ap("C3", 0, 64), 4.0, ADD)
-    ts(ap("k2I"), ap("IC", 0, 128), 1, AND); ts(ap("s3F"), ap("sF"), 7.5, GT)
-    ts(ap("pz"), ap("k2I"), ap("s3F"), NE, 4194304.0, MUL)
-    ts(ap("t256", 0, 128), ap("IC", 0, 128), 5, SHR); ts(ap("tmpA"), ap("t256", 0, 128), 12.0, ADD, 16.0, MUL); tt(ap("MP"), ap("pz"), ap("tmpA"), ADD)
-    ts(ap("t256", 128, 256), ap("IC", 0, 128), 3, SHR); ts(ap("tmpA"), ap("t256", 128, 256), 16.0, MUL); tt(ap("ML"), ap("pz"), ap("tmpA"), ADD)
-    ts(ap("MC"), ap("CG"), 16.0, MUL)
+    ts(ap("s3F"), ap("sF"), 7.5, GT)
+    put("G", lambda g: g.iota(res(ap("MP")), [[16, 16], [0, 32]], 0, 0, allow_small_or_imprecise_dtypes=True), [], [ap("MP")], 1.0)
+    put("G", lambda g: g.iota(res(ap("ML")), [[16, 16], [4, 4], [0, 4]], 0, 0, allow_small_or_imprecise_dtypes=True), [], [ap("ML")], 0.6)
+    ts(ap("k3I"), ap("IC", 0, 64), 1, AND); ts(ap("PZ"), ap("k3I"), ap("s3F"), NE, 4194304.0, MUL)
+    ts(ap("PZQ"), ap("C3", 0, 64), ap("s2F"), NE, 4194304.0, MUL)
     ts(ap("CC"), ap("IC", 0, 16), 1.0, MUL); ts(ap("CCL"), ap("IC", 0, 4), 1.0, MUL)
     ts(ap("JW0"), ap("IC", 0, 16), 16.0, MUL, ap("sF"), ADD)
     ts(ap("J256"), ap("JW0"), 256.0, ADD); ts(ap("D4096"), ap("JW0"), 4096.0, ADD)
@@ -267,8 +280,8 @@ def build(rank, core, T, topo):
     ts(ap("CL"), ap("CC"), 16.0, MUL, 15.0, ADD)
     ts(ap("oneR"), ap("CS"), -1.0, GT); ts(ap("EE", 0, 1), ap("pF"), 0.0, MUL)
     ts(ap("tmpA"), ap("CS", 0, 128), ap("sF"), LE, -1.0, MUL); tt(ap("TRIMB"), ap("tmpA"), ap("BLKB"), MUL)
-    ts(ap("IDH"), ap("IC", 0, 128), ap("pF"), EQ); cp(ap("IDB"), ap("IDH")); ts(ap("IDN"), ap("IDH"), -1.0, MUL); ts(ap("EQM"), ap("MWR"), -1.0, ADD); fill(ap("ONEB"), 1.0); fill(ap("one16"), 1.0); fill(ap("C255"), 255.0)
-    ts(ap("TRP"), ap("CS"), ap("sF"), LE, 16384.0, MUL)
+    ts(ap("IDH"), ap("IC", 0, 128), ap("pF"), EQ); cp(ap("IDB"), ap("IDH")); act(ap("ID8"), ap("IDB"), AF.Copy, scale=8192.0); ts(ap("IDN"), ap("IDH"), -1.0, MUL); ts(ap("EQM"), ap("MWR"), -1.0, ADD); fill(ap("ONEB"), 1.0); fill(ap("one16"), 1.0); fill(ap("C255"), 255.0)
+    ts(ap("TRP"), ap("CS"), ap("sF"), LE, 16384.0, MUL); ts(ap("TRH"), ap("CS"), ap("sF"), LE, 16384.0, MUL)
     ts(ap("T5"), ap("IC"), 5.0, MUL, 2.0, ADD)
     rng = []
     for c in range(16):
@@ -278,12 +291,16 @@ def build(rank, core, T, topo):
     ts(ap("kz1"), ap("T5"), -55.5, ADD, 1.0 / 112, MUL); tt(ap("KONST"), ap("kz2"), ap("kz1"), ADD)
     fill(ap("RJ", 0, 16), 300.0)
     ts(ap("IC64"), ap("IC", 0, 64), 1.0, MUL); ts(ap("PF64"), ap("IC64"), 5.0, MUL, 1280.0, ADD)
-    fill(ap("HT", 256, 768), UNF); fill(ap("lHT", 64, 128), UNF); fill(ap("RS", 64, 72), 0.0)
+    fill(ap("HT", 256, 1056), UNF); fill(ap("lHT", 64, 144), UNF); fill(ap("RS", 64, 72), 0.0)
 
     def sel(bank, o, name, lo, n):
         return [(ap(bank, o, o + n), ap("SEL", 128 * s, 128 * s + 128), ap(name, lo + s, lo + s + 16 * (n - 1) + 1, 16), s == 0, s == 15) for s in range(16)]
 
+    def pair(m):
+        return m < 14 and m not in BYS and (m ^ 1) not in BYS
+
     for t in range(RO):
+        start[0] = len(ops)
         cur, nxt = str(t % 2), str(1 - t % 2)
         cx, tx, cy, ty, wx, wy = "CX" + cur, "TX" + cur, "CX" + nxt, "TX" + nxt, "WX" + cur, "WX" + nxt
         last = t == RO - 1
@@ -316,55 +333,54 @@ def build(rank, core, T, topo):
             if mb == 0:
                 scan(ap("EE", 256, 512), ap("oneR"), ap(wx, 0, 256)); cp(ap("EE", 1, 256), ap("EE", 256, 511))
                 mm(sel("MS", 32, "EE", 0, 32))
-                ts(ap("FI"), ap("MS", 32, 64), 0.2 / 4096, MUL); ts(ap("EB"), ap("MS", 48, 64), -1.0 / 4096, MUL, 0.5, ADD)
-                ts(ap("FB"), ap("FI"), 256.0, MIN); tt(ap("FC"), ap("FB"), ap("FIX"), MAX)
-                tt(ap("NW"), ap("FC", 16, 32), ap("FC", 0, 16), SUB)
-                ts(ap("UN0"), ap("NW"), 0.0, EQ, 256.0, MUL); tt(ap("UNC"), ap("UN0"), ap("CC"), ADD)
             for m in range(4 * mb, 4 * mb + 4):
                 x, u = ap("X", 256 * m, 256 * m + 256), ind(ap("US", 0, 4096), ap("HO", 16 * m, 16 * m + 16))
                 if m in BYS:
                     act(x, u, AF.Copy)
-                elif m in (14, 15):
+                elif not pair(m):
                     tt(x, u, ap("ZB", 0, 256), SUB)
+                    if XCH and m > 2:
+                        later(x15)
+                    x15 = len(ops) - 1
                 elif m % 2 == 0:
                     tt(ap("X", 256 * m, 256 * m + 512), ind(ap("US", 0, 4096), ap("HO", 16 * m, 16 * m + 32)), ap("ZB"), SUB)
-            for m, k in (((0, 2), (2, 2)), ((0, 2), (2, 2)), ((0, 2), (2, 2)), ((0, 1), (1, 1), (2, 1), (3, 1)))[mb]:
+                    if XCH and m > 2:
+                        later(x15)
+                    x15 = len(ops) - 1
+            for m in range(4):
                 lo = 1024 * mb + 256 * m
+                k = 2 if pair(4 * mb + m) else 1
+                if k == 2 and m % 2:
+                    continue
                 if 4 * mb + m in BYS:
                     bank = BYS[4 * mb + m]
                     mm([(ap(bank, 256, 512), ap("IDB"), ap("X", lo, lo + 256), True, False), (ap(bank, 256, 512), ap("IDN"), ap("ZB", 0, 256), False, True)])
                     act(ap("A", lo, lo + 256), ap(bank, 256, 512), AF.Abs)
-                    if mb == 3:
-                        later(third)
                 else:
                     act(ap("A", lo, lo + 256 * k), ap("X", lo, lo + 256 * k), AF.Abs)
-                    if mb == 2:
-                        third = len(ops) - 1
-            d = "DA" if mb % 2 == 0 else "DB"
-            if mb < 3:
-                mm([(ap(d, 0, 64), ap("SEL", 128 * s, 128 * s + 128), ap("A", 1024 * mb + s, 1024 * mb + s + 1009, 16), s == 0, s == 15) for s in range(16)])
-                tt(ap("K", 64 * mb, 64 * mb + 64), ap(d, 0, 64), ap("MC", 64 * mb, 64 * mb + 64), ADD)
-            if mb == 1:
-                tt(ap("K2"), ap("K", 0, 64), ap("K", 64, 128), MIN)
-            if mb == 2:
-                tt(ap("K3"), ap("K2"), ap("K", 128, 192), MIN); tt(ap("K5"), ap("K3", 0, 32), ap("K3", 32, 64), MIN)
-        for h in (0, 1):
-            d, lo = ("DB", "DA")[h], 3072 + 512 * h
-            mm([(ap(d, 128, 192), ap("SLP", 128 * r, 128 * r + 128), ap("A", lo + r, lo + 512, 8), r == 0, r == 7) for r in range(8)])
-            kp = ap("KP", 64 * h, 64 * h + 64)
-            tt(kp, ap(d, 128, 192), ap("MP", 64 * h, 64 * h + 64), ADD)
-            kq = ap("KQ", 32 * h, 32 * h + 32)
-            tt(kq, ap("KP", 64 * h, 64 * h + 63, 2), ap("KP", 64 * h + 1, 64 * h + 64, 2), MIN)
-            tt(ap("K6" if h == 0 else "K7"), ap("K5" if h == 0 else "K6"), kq, MIN)
-        ts(ap("HT", 0, 256), ap("HI"), -2047.0, ADD)
-        tt(ap("KEY"), ap("K7", 0, 16), ap("K7", 16, 32), MIN)
+        ts(ap("RM", 0, 64), ap("IC64"), 0.0, MUL, b16, ADD)
+        for n, h in enumerate(HB):
+            d, lo = ("DA", "DB")[n % 2], 512 * h
+            mm([(ap(d, 0, 64), ap("IDB"), ap("MP", 64 * h, 64 * h + 64), True, False), (ap(d, 0, 64), ap("IDB"), ap("PZ"), False, False)] +
+               [(ap(d, 0, 64), ap("SLP", 128 * r, 128 * r + 128), ap("A", lo + r, lo + 512, 8), False, r == 7) for r in range(8)])
+            tt(ap("RM", 64 * n + 64, 64 * n + 128), ap(d, 0, 64), ap("RM", 64 * n, 64 * n + 64), MIN)
+        ts(ap("HT", 0, 256), ap("HI"), -2047.0, ADD); later(x15)
+        tt(ap("KQ"), ap("RM", 512, 575, 2), ap("RM", 513, 576, 2), MIN)
+        tt(ap("KEY"), ap("KQ", 0, 16), ap("KQ", 16, 32), MIN)
+        ts(ap("FI"), ap("MS", 32, 64), 0.2 / 256, MUL); later(x15); ts(ap("EB"), ap("MS", 48, 64), -1.0 / 256, MUL, 0.5, ADD); later(x15)
+        ts(ap("FB"), ap("FI"), 256.0, MIN); tt(ap("FC"), ap("FB"), ap("FIX"), MAX)
+        tt(ap("NW"), ap("FC", 16, 32), ap("FC", 0, 16), SUB)
+        ts(ap("UN0"), ap("NW"), 0.0, EQ, 512.0, MUL); tt(ap("UNC"), ap("UN0"), ap("CC"), ADD)
+        if t:
+            ts(ind(ap(cx), ap("OBU")), ap("IC64"), 1.0, MUL, float(S + CAP * (t - 1)), ADD); later(x15)
+            dma(ext("yc", L * (t - 1), L * t), ap(cx, 0, 256, 1, slice(0, 128, 16)), 2.0)
         fill(ap("ZA", 0, 64), 1024.0)
         ts(ap("PO"), ap("KEY"), b16, GE); tt(ap("PN"), ap("PO"), ap("NW"), MUL); scan(ap("SC"), ap("one16"), ap("PN"))
+        scn = len(ops) - 1
         ts(ap("UA"), ap("PN"), 0.5, LT); tt(ap("PEN"), ap("UA"), ap("J256"), MUL)
         pen = len(ops) - 1
         mm([(ap("MS", 64, 80), ap("TRIMB"), ap("PN"), True, False), (ap("MS", 64, 80), ap("BLKB"), ap("SC"), False, False), (ap("MS", 64, 80), ap("IDH"), ap("PEN"), False, True)])
         cp(ap("OF"), ap("MS", 64, 80))
-        cp(ind(ap("ZA"), ap("OF")), ap("ZB", 0, 256))
         lender = T.cores[(rank + 1 + t % 3) % 4]
         borrower = T.cores[(rank - 1 - t % 3) % 4]
 
@@ -377,31 +393,40 @@ def build(rank, core, T, topo):
             ops[-1]["n"] = len(topo.engines(core, dst)[:8])
             put("N", None, [], [ap(o)], FLIGHT, sem=sem, inc=8)
             ops[-1]["after"] = [len(ops) - 2]
-        send("ZL%d" % t, ap("ZA", 0, 64), "ask%d" % t, "la", lender)
         if not last:
             bn = "b16a" if t % 2 == 0 else "b16b"
             mm([(ap("MS", 96, 97), ap("ONEB"), ap("SC", 15, 16), True, True)])
-            cp(ap("PPI"), ap("MS", 96, 97)); ts(ap("PPJ"), ap("PPI"), 63, AND); ts(ap(bn), ap("PPJ"), 256.0, MUL, ap("th16"), ADD)
-        cp(ap("KI"), ap("KEY")); later(pen); ts(ap("MI"), ap("KI"), 240, AND)
-        ts(ap("LA"), ap("PO"), 256.0, MUL); later(pen); tt(ap("LC"), ap("LA"), ap("UNC"), ADD); tt(ap("LD"), ap("LC"), ap("MI"), ADD); cp(ap("LL"), ap("LD"))
-        tt(ap("HM"), ind(ap("HT"), ap("LL")), ap("MWR"), MUL); later(pen)
+            cp(ap("PPI"), ap("MS", 96, 97)); ts(ap("PPJ"), ap("PPI"), 63, AND); ts(ap(bn), ap("PPJ"), 512.0, MUL, ap("th16"), ADD)
+        ts(ap("MI"), ap("KEY"), 511, AND); tt(ap("LD"), ap("MI"), ap("UNC"), ADD); cp(ap("LL"), ap("LD"))
+        tt(ap("HM"), ind(ap("HT"), ap("LL")), ap("MWR"), MUL); later(pen); later(scn)
         scan(ap("HS"), ap("RST"), ap("HM"))
         mm([(ap("HR", 0, 256), ap("BLKH"), ap("HM"), True, True)])
         cp(ap("HRH"), ap("HR", 0, 256))
         act(ap(cx, 256, 512), ap("HR", 0, 256), AF.Copy, bias=2047.0)
-        ts(ap("HW"), ap("HS", 15, 256, 16), 2047.0, ADD); tt(ap("HN"), ap("HW"), ap("D4096"), SUB); cp(ap("HL"), ap("HW"))
-        ts(ap("HG"), ap("HW"), 0.0, GE); tt(ap("HD"), ap("HG"), ap("HN"), MUL)
+        ts(ap("HW"), ap("HS", 15, 256, 16), 2047.0, ADD); cp(ap("HL"), ap("HW"))
+        mm([(ap("DA", 256, 512), ap("BLKH"), ap("HM"), True, False), (ap("DA", 256, 512), ap("IDH"), ap("TRH"), False, True)])
+        act(ap("HRT"), ap("DA", 256, 512), AF.Copy)
+        ts(ap("UR"), ap("HRH"), UNF, EQ)
+        mm([(ap("CT", 0, 256), ap("ID8"), ap("UR"), True, False), (ap("CT", 0, 256), ap("IDB"), ap("NM"), False, False)])
         for c in range(15):
             ts(ap("ET", 256 * c, 256 * c + 240 - 16 * c), ap("HRH", 16 * c + 16, 256), ap("HS", 16 * c + 15, 16 * c + 16), EQ)
-            mm([(ap("CT", 16 * c + 16, 256), ap("BLKB"), ap("ET", 256 * c, 256 * c + 240 - 16 * c), c == 0, False)])
-        et = len(ops) - 2
-        tt(ap("HRT"), ap("HR", 0, 256), ap("TRP"), ADD); later(et)
+            if c <= NET:
+                later(len(ops) - 3)
+            mm([(ap("CT", 16 * c + 16, 256), ap("BLK8"), ap("ET", 256 * c, 256 * c + 240 - 16 * c), False, False)])
+            if c == max(NET, 0):
+                net = len(ops) - 2
+                cp(ind(ap("ZA"), ap("OF")), ap("ZB", 0, 256))
+                if NET >= 0:
+                    later(net)
+                send("ZL%d" % t, ap("ZA", 0, 64), "ask%d" % t, "la", lender)
         tt(ap("ET", 3840, 4096), ind(ap("HS"), ap("CL")), ap("HRT"), EQ)
-        mm([(ap("CT", 16, 256), ap("BLKB"), ap("ET", 3856, 4096), False, True), (ap("CT", 0, 16), ap("BLKB"), ap("ET", 3840, 3856), True, True)])
+        mm([(ap("CT", 0, 256), ap("BLK8"), ap("ET", 3840, 4096), False, True)])
         ctl = len(ops) - 1
-        ts(ap("UR"), ap("HRH"), UNF, EQ, -1.0, MUL)
-        tt(ap("WM"), ap("CT", 0, 256), ap("EQM"), EQ); scan(ap("WS"), ap("RST"), ap("WM"))
-        tt(ap("LO1"), ap("WS", 15, 256, 16), ap("HD"), MUL); tt(ap("LO2"), ap("LO1"), ap("D4096"), ADD); cp(ap("LO"), ap("LO2"))
+        scan(ap("WS"), ap("RSTB"), ap("CT", 0, 256), ADD, MIN)
+        act(ap("WD"), ap("CT", 0, 256), AF.Relu, bias=1.0, scale=-1.0)
+        mm([(ap("MS", 256, 512), ap("BLKB"), ap("WD"), True, True)])
+        act(ap("WN"), ap("MS", 256, 512), AF.Copy)
+        tt(ap("LO1"), ap("WS", 15, 256, 16), ap("HW"), ADD); tt(ap("LO2"), ap("LO1"), ap("D4096"), MIN); cp(ap("LO"), ap("LO2"))
         cp(ind(ap("US"), ap("LO")), ap("C255"))
         zl = "ZL%d" % t
         lst = []
@@ -421,40 +446,40 @@ def build(rank, core, T, topo):
         cp(ap("lUQ"), ap("lUVA"))
         for c in range(4):
             ts(ap("lHV", c, 64, 4), ap("KR"), ap("lUQ", c, c + 1), MUL, ap("lUQ", 4 + c, 5 + c), ADD)
-        ts(ap("lHI"), ap("lHV"), 4095, AND); cp(ap("lHO"), ap("lHI")); ts(ap("lHT", 0, 64), ap("lHI"), -2047.0, ADD)
+        ts(ap("lHI"), ap("lHV"), 4095, AND); cp(ap("lHO"), ap("lHI"));
         for mb in range(4):
-            x, u = ap("lX", 256 * mb, 256 * mb + 256), ind(ap("US", 0, 4096), ap("lHO", 16 * mb, 16 * mb + 16))
-            if mb == 3:
-                act(x, u, AF.Copy)
-            else:
-                tt(x, u, ap("ZT"), SUB)
-                lx = len(ops) - 1
-        mm([(ap("ZP", 256, 512), ap("IDB"), ap("lX", 768, 1024), True, False), (ap("ZP", 256, 512), ap("IDN"), ap("ZT"), False, True)])
+            w = 256 if mb < 3 else 128
+            tt(ap("lX", 256 * mb, 256 * mb + w), ind(ap("US", 0, 4096), ap("lHO", 16 * mb, 16 * mb + w // 16)), ap("ZT", 0, w), SUB)
+            lx = len(ops) - 1
+        act(ap("lX", 896, 1024), ind(ap("US", 0, 4096), ap("lHO", 56, 64)), AF.Copy)
+        mm([(ap("ZP", 256, 384), ap("IDB"), ap("lX", 896, 1024), True, False), (ap("ZP", 256, 384), ap("IDN"), ap("ZT", 0, 128), False, True)])
+        ts(ap("lHT", 0, 64), ap("lHI"), -2047.0, ADD); later(lx)
         for mb in range(3):
             act(ap("lA", 256 * mb, 256 * mb + 256), ap("lX", 256 * mb, 256 * mb + 256), AF.Abs)
-        act(ap("lA", 768, 1024), ap("ZP", 256, 512), AF.Abs)
-        for h in (0, 1):
-            d = ("DB", "DA")[h]
-            mm([(ap(d, 64, 128), ap("SLP", 128 * r, 128 * r + 128), ap("lA", 512 * h + r, 512 * h + 512, 8), r == 0, r == 7) for r in range(8)])
-            tt(ap("lK", 64 * h, 64 * h + 64), ap(d, 64, 128), ap("ML", 64 * h, 64 * h + 64), ADD)
-        tt(ap("lK0"), ap("lK", 0, 64), ap("lK", 64, 128), MIN)
-        tt(ap("lK1"), ap("lK0", 0, 32), ap("lK0", 32, 64), MIN); tt(ap("lK2"), ap("lK1", 0, 16), ap("lK1", 16, 32), MIN)
-        tt(ap("lK3"), ap("lK2", 0, 8), ap("lK2", 8, 16), MIN); tt(ap("lKEY"), ap("lK3", 0, 7, 2), ap("lK3", 1, 8, 2), MIN)
-        ts(ap("lPO"), ap("lKEY"), b16, GE, 64.0, MUL); tt(ap("lLC"), ap("lPO"), ap("CCL"), ADD)
-        cp(ap("lKI"), ap("lKEY")); ts(ap("lMI"), ap("lKI"), 2, SHR, 60, AND)
-        tt(ap("lLD"), ap("lLC"), ap("lMI"), ADD); cp(ap("lLL"), ap("lLD"))
+        act(ap("lA", 896, 1024), ap("ZP", 256, 384), AF.Abs)
+        act(ap("lA", 768, 896), ap("lX", 768, 896), AF.Abs)
+        ts(ap("lRM", 0, 64), ap("IC64"), 0.0, MUL, b16, ADD)
+        for n, h in enumerate((0, 1, 2, 3)):
+            d = ("DA", "DB")[n % 2]
+            mm([(ap(d, 64, 128), ap("IDB"), ap("ML", 64 * h, 64 * h + 64), True, False), (ap(d, 64, 128), ap("IDB"), ap("PZQ"), False, False)] +
+               [(ap(d, 64, 128), ap("SLQ", 128 * r, 128 * r + 128), ap("lA", 256 * h + r, 256 * h + 256, 4), False, r == 3) for r in range(4)])
+            tt(ap("lRM", 64 * n + 64, 64 * n + 128), ap(d, 64, 128), ap("lRM", 64 * n, 64 * n + 64), MIN)
+        tt(ap("lK1"), ap("lRM", 256, 288), ap("lRM", 288, 320), MIN); tt(ap("lK2"), ap("lK1", 0, 16), ap("lK1", 16, 32), MIN)
+        tt(ap("lK3"), ap("lK2", 0, 16, 2), ap("lK2", 1, 16, 2), MIN); tt(ap("lKEY"), ap("lK3", 0, 8, 2), ap("lK3", 1, 8, 2), MIN)
+        ts(ap("lMI"), ap("lKEY"), 2, SHR, 127, AND); cp(ap("lLL"), ap("lMI"))
         tt(ap("lHM"), ind(ap("lHT"), ap("lLL")), ap("MWR", 0, 64), MUL)
         scan(ap("lHS"), ap("RST", 0, 64), ap("lHM"))
         mm([(ap("HR", 256, 320), ap("BLKH"), ap("lHM"), True, True)])
-        cp(ap("lHRH"), ap("HR", 256, 320)); tt(ap("lHRT"), ap("HR", 256, 320), ap("TRP", 0, 64), ADD)
+        tt(ap("lHRT"), ap("HR", 256, 320), ap("TRP", 0, 64), ADD)
         ts(ap("lHW"), ap("lHS", 15, 64, 16), 2047.0, ADD); tt(ap("lHD"), ap("lHW"), ap("D4096", 0, 4), SUB); cp(ap("lHL"), ap("lHW"))
-        ts(ap("lET", 256, 320), ap("lHRH"), UNF, EQ)
+        ts(ap("lET", 256, 320), ap("HR", 256, 320), UNF, EQ)
         mm([(ap("CT", 256, 320), ap("BLKB"), ap("lET", 256, 320), True, False)])
         for c in range(3):
-            ts(ap("lET", 64 * c, 64 * c + 48 - 16 * c), ap("lHRH", 16 * c + 16, 64), ap("lHS", 16 * c + 15, 16 * c + 16), EQ)
+            ts(ap("lET", 64 * c, 64 * c + 48 - 16 * c), ap("HR", 272 + 16 * c, 320), ap("lHS", 16 * c + 15, 16 * c + 16), EQ)
             mm([(ap("CT", 272 + 16 * c, 320), ap("BLKB"), ap("lET", 64 * c, 64 * c + 48 - 16 * c), False, False)])
         tt(ap("lET", 192, 256), ind(ap("lHS"), ap("CL", 0, 4)), ap("lHRT"), EQ)
         mm([(ap("CT", 256, 320), ap("BLKB"), ap("lET", 192, 256), False, True)])
+        lct = len(ops) - 1
         ts(ap("GR"), ap("CT", 256, 320), 0.0, EQ)
         tt(ap("RS", 0, 64), ind(ap("TP"), ap("lHL")), ap("GR"), MUL)
         tt(ap("GM"), ap("CT", 256, 320), ap("EQM", 0, 64), EQ); scan(ap("GS"), ap("RST", 0, 64), ap("GM"))
@@ -474,12 +499,13 @@ def build(rank, core, T, topo):
             off += (hi - lo + 15) // 16 * 16
         act(ap("RJ", 1, 257), ap("JP", 0, 256), AF.Relu, bias=254.0, scale=-0.5)
         mm(sel("JP", 256, "RJ", 1, 16)); later(ctl); later(luv)
-        ts(ap("JW"), ap("JP", 256, 272), -1.0 / 4096, MUL, 254.0, ADD); cp(ap("JL"), ap("JW"))
-        tt(ap("WN"), ap("CT", 0, 256), ap("UR"), EQ); later(lx)
-        tt(ap("FIRST"), ap("RJ", 1, 257), ap("RJ", 0, 256), NE); later(lx)
+        ts(ap("JW"), ap("JP", 256, 272), -1.0 / 256, MUL, 254.0, ADD); later(lx); cp(ap("JL"), ap("JW"))
+        mm([(ap("MS", 256, 512), ap("IDB"), ap("RJ", 0, 256), True, False), (ap("MS", 256, 512), ap("IDN"), ap("RJ", 1, 257), False, True)]); later(luv)
+        act(ap("FIRST"), ap("MS", 256, 512), AF.Sign)
         tt(ap("FW"), ind(ap("WN"), ap("JL")), ap("FIRST"), MUL); later(lx)
-        mm(sel("JP", 272, "FW", 0, 16))
-        ts(ap("LB"), ap("JP", 272, 288), 1.0 / 16, MUL); tt(ap("JX"), ap("LB"), ap("JW"), ADD); cp(ap("JL2"), ap("JX"))
+        mm(sel("JP", 272, "FW", 0, 16)); later(lct)
+        tt(ap("JX"), ap("JP", 272, 288), ap("JW"), ADD); cp(ap("JL2"), ap("JX"))
+        jl2 = len(ops) - 1
         if not last:
             act(ap(tx, 256, 512), ind(ap("TP"), ap("HL")), AF.Copy)
             act(ap(wx, 256, 512), ind(ap("WTAB"), ap("HL")), AF.Copy)
@@ -487,21 +513,22 @@ def build(rank, core, T, topo):
             act(ap(wy, 0, 256), ind(ap(wx, 0, 512), ap("JL2")), AF.Copy)
         act(ap(cy, 0, 256), ind(ap(cx, 0, 512), ap("JL2")), AF.Copy)
         act(ap("EA", 0, 64), ap("PF64"), AF.Copy)
-        cp(ind(ap("EA"), ap("OF")), ap("EE", 0, 256)); later(lend)
+        cp(ind(ap("EA"), ap("OF")), ap("EE", 0, 256)); later(lend); later(jl2)
         tt(ap("EM"), ap("EA", 0, 64), ap("MWR", 0, 64), MUL); scan(ap("EQ"), ap("RST", 0, 64), ap("EM"))
         ts(ap("FAI"), ap("EQ", 15, 64, 16), 0.2, MUL); cp(ap("FA"), ap("FAI"))
         rb = "RB%d" % t
         tt(ap("OB"), ap(rb, 64, 68), ap("FA"), ADD); cp(ap("OBU"), ap("OB"))
         if not last:
             cp(ind(ap(ty), ap("OBU")), ap(rb, 0, 64)); cp(ind(ap(wy), ap("OBU")), ap("W64"))
-        ts(ind(ap(cy), ap("OBU")), ap("IC64"), 1.0, MUL, float(S + CAP * t), ADD)
         dma(ext("yu", S + CAP * t, S + CAP * t + CAP), ap("RV%d" % t), 2.0)
-        dma(ext("yc", L * t, L * t + L), ap(cy, 0, 256, 1, slice(0, 128, 16)), 2.0)
+        if last:
+            ts(ind(ap(cy), ap("OBU")), ap("IC64"), 1.0, MUL, float(S + CAP * t), ADD)
+            dma(ext("yc", L * t, L * t + L), ap(cy, 0, 256, 1, slice(0, 128, 16)), 2.0)
     dma(ext("yu", 0, S), ap("US", 0, 4096), 6.0)
     return ops
 
 
-def order(ops):
+def order(ops, noise=None):
     last = {}
     for i, o in enumerate(ops):
         pre = {}
@@ -548,6 +575,8 @@ def order(ops):
     pri = [0.0] * n
     for i in range(n - 1, -1, -1):
         pri[i] = ops[i]["c"] + max([pri[k] + HOP for k in succ[i]], default=0.0)
+    if noise is not None:
+        pri = [pri[i] + noise[ops[i]["k"]] for i in range(n)]
     left = [len(o["pre"]) for o in ops]
     ready = {}
     est = [0.0] * n
@@ -567,6 +596,11 @@ def order(ops):
             c = [i for i in lst if max(f, est[i]) <= m + 0.03]
             b = max(c, key=lambda i: pri[i])
             tm = max(f, est[b])
+            h = max((i for i in lst if est[i] <= tm + AHEAD), key=lambda i: pri[i]) if AHEAD else b
+            if pri[h] > pri[b] + 0.5 and est[h] > tm and tm + ops[b]["c"] > est[h] + 0.02 and q != "N":
+                c = [i for i in lst if max(f, est[i]) + ops[i]["c"] <= est[h] + 0.02]
+                b = max(c, key=lambda i: pri[i]) if c else h
+                tm = max(f, est[b])
             if best is None or tm < best[0]:
                 best = (tm, q, b)
         tm, q, b = best

import math
from concourse.mybir import dt, AluOpType, AxisListType, ActivationFunctionType
import comms_topo

RO, L, S, CAP = 6, 256, 4096, 64
UNF = -2048.0

_B = {}


def _b(name, cols, dtype, rows=128):
    _B[name] = ("sbuf", [rows, cols], dtype)


F, BF, H, I, U16 = "float32", "bfloat16", "float16", "int32", "uint16"
_b("US", 4352, BF); _b("TP", 4096, BF)
_b("c8", 256, I, 8); _b("hwi", 2, I); _b("kmi", 1, I); _b("th8", 1, I, 8)
_b("c8h", 256, H, 8); _b("th8h", 1, H, 8); _b("hwf", 2, F); _b("hwg", 2, F); _b("hwh", 2, H); _b("wl", 2, F); _b("wr", 2, F); _b("ws", 2, F)
_b("kh", 16, H); _b("KR", 16, F); _b("th16", 1, F); _b("b16a", 1, F); _b("b16b", 1, F); _b("ksc", 1, F)
_b("IC", 256, I); _b("pI", 1, I); _b("sI", 1, I); _b("gI", 1, I); _b("s8I", 1, I); _b("s2I", 1, I)
_b("pF", 1, F); _b("sF", 1, F); _b("gF", 1, F); _b("s8F", 1, F); _b("s2F", 1, F); _b("sge8", 1, F); _b("slt8", 1, F)
_b("CS", 256, I); _b("CG", 256, I); _b("C3", 128, I); _b("CSB", 128, BF); _b("CQB", 128, BF); _b("tmpA", 128, F); _b("tmpB", 128, F)
_b("MWR", 256, F); _b("RST", 256, F); _b("BLKH", 128, H); _b("BLKB", 128, BF); _b("ONEB", 128, BF); _b("IDH", 128, H); _b("IDB", 128, BF); _b("IDN", 128, BF); _b("EQM", 256, F)
_b("TRIMB", 128, BF); _b("PL", 128, BF); _b("PR", 128, BF); _b("PH", 128, H); _b("SEL", 2048, BF); _b("REP8", 128, H, 8)
_b("WT", 24 * 128, H); _b("MQ", 128, F); _b("MC", 256, F); _b("MCL", 64, F); _b("t256", 256, I); _b("TRP", 256, F)
_b("C255", 256, BF); _b("T5", 256, F); _b("KONST", 256, BF); _b("one16", 16, F); _b("oneR", 256, H); _b("CC", 16, F); _b("JW0", 16, F); _b("jI", 16, I)
_b("J256", 16, F); _b("D4096", 16, F); _b("FIX", 32, F); _b("CLf", 16, F); _b("CL", 16, U16); _b("IC64", 64, F); _b("PF64", 64, F); _b("CCL", 4, F)
for _k in "01":
    _b("CX" + _k, 640, F); _b("TX" + _k, 640, BF); _b("WX" + _k, 640, BF)
_b("WTAB", 4096, BF); _b("W64", 64, BF); _b("B256", 128, BF); _b("rsc", 1, F); _b("rs1", 1, F); _b("rs2", 1, F); _b("rs3", 1, F)
_b("CM", 256, F); _b("CM2", 256, F); _b("CL0", 16, U16)
_b("ZB", 512, BF); _b("UVM", 128, F); _b("UT", 64, F); _b("UVI", 32, I); _b("UVA", 32, I); _b("UVW", 16, I); _b("UQ", 32, F)
_b("HV", 256, I); _b("HF", 64, F); _b("HI", 256, I); _b("HO", 256, U16); _b("HT", 1056, F)
_b("X", 4096, BF); _b("A", 4096, BF); _b("K", 256, F); _b("K2", 64, F); _b("K3", 64, F); _b("K5", 32, F); _b("RM", 576, F); _b("KQ", 32, F); _b("MP", 512, BF); _b("k3I", 64, I); _b("PZ", 64, BF); _b("PZQ", 64, BF); _b("SLQ", 512, BF); _b("B512", 128, BF); _b("lRM", 320, F); _b("ML", 256, BF); _b("SLP", 1024, BF); _b("s3F", 1, F); _b("k2I", 128, I); _b("pz", 128, F); _b("kz1", 256, I); _b("kz2", 256, F); _b("C7B", 128, BF); _b("TRH", 256, H); _b("BLK8", 128, BF); _b("ID8", 128, BF); _b("NM", 256, BF); _b("RSTB", 256, F); _b("WD", 256, BF); _b("UR", 256, BF); _b("KEY", 16, I)
_b("PO", 16, F); _b("PN", 16, BF); _b("SC", 16, BF); _b("UA", 16, F); _b("PEN", 16, H); _b("OF", 16, U16); _b("ZA", 768, BF)
_b("PPI", 1, I); _b("PPJ", 1, I); _b("PPF", 1, F)
_b("KI", 16, I); _b("MI", 16, I); _b("LA", 16, F); _b("LB", 16, F); _b("LC", 16, F); _b("LD", 16, F); _b("LL", 16, U16)
_b("HM", 256, H); _b("HS", 256, F); _b("HRH", 256, H); _b("HRT", 256, F); _b("HW", 16, F); _b("HD", 16, F); _b("HL", 16, U16)
_b("ET", 17 * 256, BF); _b("WN", 256, BF); _b("WM", 256, F); _b("WS", 256, F); _b("LO1", 16, F); _b("LO2", 16, F); _b("LO", 16, U16)
_b("CI", 256, I); _b("CI3", 256, I); _b("W16", 256, H); _b("EE", 512, H); _b("FI", 32, I); _b("FB", 32, F); _b("FC", 32, F); _b("NW", 16, F); _b("UN0", 16, F); _b("UNC", 16, F)
_b("EB", 16, F); _b("SG", 4096, BF); _b("RJ", 272, BF); _b("FIRST", 256, BF); _b("JW", 16, F); _b("JL", 16, U16); _b("FW", 256, BF); _b("JX", 16, F); _b("JL2", 16, U16)
_b("EA", 768, F); _b("EM", 64, F); _b("EQ", 64, F); _b("FAI", 4, I); _b("FA", 4, F); _b("OB", 4, F); _b("OBU", 4, U16)
for _k in range(RO):
    _b("ZL%d" % _k, 64, BF); _b("RB%d" % _k, 72, BF); _b("RV%d" % _k, 64, BF)
_b("ZT", 256, BF); _b("lUVM", 32, F); _b("lUT", 16, F); _b("lUVI", 8, I); _b("lUVA", 8, I); _b("lUVW", 4, I); _b("lUQ", 8, F)
_b("lHV", 64, I); _b("lHI", 64, I); _b("lHO", 64, U16); _b("lHT", 144, F); _b("lX", 1024, BF); _b("lA", 1024, BF)
_b("lK", 128, F); _b("lK0", 64, F); _b("lK1", 32, F); _b("lK2", 16, F); _b("lK3", 8, F); _b("lKEY", 4, I); _b("lKI", 4, I); _b("lMI", 4, I); _b("lPO", 4, F); _b("lLA", 4, F); _b("lLB", 4, F)
_b("lLC", 4, F); _b("lLD", 4, F); _b("lLL", 4, U16); _b("lHM", 64, H); _b("lHS", 64, F); _b("lHRH", 64, H); _b("lHRT", 64, F); _b("lHW", 4, F); _b("lHD", 4, F); _b("lHL", 4, U16)
_b("lET", 320, BF); _b("GR", 64, BF); _b("GM", 64, F); _b("GS", 64, F); _b("RS", 72, BF); _b("RSU", 64, BF); _b("lO1", 4, F); _b("lO2", 4, F); _b("lLO", 4, U16)
_PS = ["UVP", "ZP", "DA", "DB", "HR", "CT", "MS", "JP"]
_SIZE = {F: 4, BF: 2, H: 2, I: 4, U16: 2}
_OWN = ("US", "TP", "X", "A", "ZA")
NET = 0
XCH = False
HB = (0, 1, 2, 3, 4, 6, 5, 7)
BYS = {3: "ZP", 7: "CT", 13: "ZP"}
SCRATCH = {}
_AT = {}
_fill = {}
for _n, (_w, _sh, _d) in _B.items():
    if _n in _OWN or _n[:2] in ("ZL", "RB", "RV") or _n in ("RS", "RSU") or _sh[0] != 128:
        SCRATCH[_n] = (_w, _sh, _d); _AT[_n] = (_n, 0)
    else:
        _q = 32 // _SIZE[_d]
        _AT[_n] = ("ar_" + _d, _fill.get(_d, 0))
        _fill[_d] = _fill.get(_d, 0) + (_sh[1] + _q - 1) // _q * _q
for _d, _c in _fill.items():
    SCRATCH["ar_" + _d] = ("sbuf", [128, _c], _d)
for _n in _PS:
    SCRATCH[_n] = ("psum", [128, 512], F); _AT[_n] = (_n, 0); _B[_n] = SCRATCH[_n]
ND = 24
SEMAPHORES = ["sV", "sS", "sP", "sG", "la", "lr", "lu"] + ["reu%d" % k for k in range(RO)] + ["ask%d" % k for k in range(RO)] + ["rep%d" % k for k in range(RO)] + ["d%d" % k for k in range(ND)]

CY = 0.001
GA, SCT = 1.56, 3.8
HOP, OWN = 0.10, 0.05
FLIGHT = 2.8
AHEAD = 0.0


def build(rank, core, T, topo):
    ops = []
    start = [-1000]

    def ap(name, lo=0, hi=None, st=1, rows=None):
        hi = _B[name][1][1] if hi is None else hi
        return ("a", name, lo, hi, st, rows)

    def ind(win, off):
        return ("i", win, off)

    def ext(name, lo, hi):
        return ("x", name, lo, hi)

    def res(d):
        if d[0] == "i":
            return res(d[1]).indirect(res(d[2]))
        if d[0] == "x":
            return T[d[1]][:, d[2]:d[3]]
        _, name, lo, hi, st, rows = d
        t, off = _AT[name]
        n = _B[name][1][0]
        rs = slice(0, n) if rows is None else rows
        return T[t][rs, off + lo:off + hi] if st == 1 else T[t][rs, off + lo:off + hi:st]

    def acc(d):
        if d[0] == "x":
            return []
        if d[0] == "i":
            return acc(d[1]) + acc(d[2])
        return [(d[1], d[2], d[3], d[4])]

    def n_of(d):
        return 16 * n_of(d[2]) if d[0] == "i" else (d[3] - d[2] + d[4] - 1) // d[4]

    def size(d):
        return _SIZE[_B[d[1]][2]]

    def isps(d):
        return d[0] == "a" and d[1] in _PS

    def put(q, fn, reads, writes, cost, sem=None, inc=1):
        R, W = [], []
        for d in reads:
            R += acc(d)
        for d in writes:
            if d[0] == "i":
                W += acc(d[1]); R += acc(d[2])
            else:
                W += acc(d)
        ops.append({"q": q, "fn": fn, "R": R, "W": W, "c": cost, "sem": sem, "inc": inc, "k": len(ops) - start[0]})

    class V:
        pass

    from_ops = AluOpType

    def vcost(n, full, inds, outs_ind):
        if outs_ind:
            return 0.06 + n * SCT * CY
        if inds:
            return 0.06 + n * GA * CY
        return max(64, n * full) * CY

    def sc(x):
        return res(x) if isinstance(x, tuple) else x

    def tt(o, a, b, op):
        full = 1 if isps(a) or isps(b) else 2
        put("V", lambda g: g.vector.tensor_tensor(res(o), res(a), res(b), op), [a, b], [o], vcost(n_of(o), full, a[0] == "i", o[0] == "i"))

    def ts(o, a, s1, op0, s2=None, op1=None):
        two = 0.5 if not isps(a) and not isps(o) and o[0] == "a" and size(a) == 2 and size(o) == 2 else 1
        rd = [a] + [x for x in (s1, s2) if isinstance(x, tuple)]
        if op1 is None:
            put("V", lambda g: g.vector.tensor_scalar(res(o), res(a), sc(s1), None, op0), rd, [o], vcost(n_of(o), two, a[0] == "i", o[0] == "i"))
        else:
            put("V", lambda g: g.vector.tensor_scalar(res(o), res(a), sc(s1), sc(s2), op0, op1), rd, [o], vcost(n_of(o), two, a[0] == "i", o[0] == "i"))

    def cp(o, a):
        two = 0.5 if a[0] == "a" and o[0] == "a" and not isps(a) and size(a) == 2 and size(o) == 2 else 1
        put("V", lambda g: g.vector.tensor_copy(res(o), res(a)), [a], [o], vcost(n_of(o), two, a[0] == "i", o[0] == "i"))

    def scan(o, a, b, op0=AluOpType.mult, op1=AluOpType.add):
        put("V", lambda g: g.vector.tensor_tensor_scan(res(o), res(a), res(b), 0.0, op0, op1), [a, b], [o], vcost(n_of(o), 1, False, False))

    def fill(o, v):
        put("V", lambda g: g.vector.memset(res(o), v), [], [o], vcost(n_of(o), 0.5, False, False))

    def act(o, a, func, bias=0.0, scale=1.0):
        rd = [a] + [x for x in (bias, scale) if isinstance(x, tuple)]
        put("S", lambda g: g.scalar.activation(res(o), res(a), func, bias=sc(bias), scale=sc(scale)), rd, [o],
            0.08 + n_of(o) * (GA if a[0] == "i" else 1) * CY)

    def mm(lst):
        def fn(g):
            r = None
            for o, l, rh, st, sp in lst:
                r = g.tensor.matmul(res(o), res(l), res(rh), st, sp)
            return r
        put("P", fn, [x[1] for x in lst] + [x[2] for x in lst], [x[0] for x in lst], sum(max(64, n_of(x[2])) for x in lst) * CY)

    def later(k):
        ops[-1].setdefault("after", []).append(k)

    nd = [0]

    def dma(o, a, cost):
        k = "d%d" % nd[0]; nd[0] += 1
        put("Y", lambda g: g.sync.dma_start(res(o) if isinstance(o, tuple) else o, res(a) if isinstance(a, tuple) else a),
            [a] if isinstance(a, tuple) else [], [o] if isinstance(o, tuple) else [], cost, sem=k, inc=16)

    ADD, SUB, MUL, MIN, MAX = from_ops.add, from_ops.subtract, from_ops.mult, from_ops.min, from_ops.max
    EQ, NE, GE, GT, LT, LE = from_ops.is_equal, from_ops.not_equal, from_ops.is_ge, from_ops.is_gt, from_ops.is_lt, from_ops.is_le
    SHR, AND = from_ops.arith_shift_right, from_ops.bitwise_and
    AF = ActivationFunctionType

    dma(ap("c8"), T.c0[:, :], 2.0); dma(ap("hwi"), T.hw[:, :], 2.0); dma(ap("kmi"), T.km[:, :], 2.0); dma(ap("th8"), T.th[:, :], 2.0)
    dma(ap("TP"), ext("tp", 0, 4096), 6.0)
    for k in range(4):
        later(k)
    dma(ap("US", 0, 4096), ext("us", 0, 4096), 8.0); later(4)

    put("G", lambda g: g.iota(res(ap("pI")), [[0, 1]], 0, 1), [], [ap("pI")], 0.2)
    put("G", lambda g: g.iota(res(ap("IC")), [[1, 256]], 0, 0), [], [ap("IC")], 0.6)
    ts(ap("sI"), ap("pI"), 15, AND); ts(ap("gI"), ap("pI"), 4, SHR); ts(ap("s2I"), ap("sI"), 2, SHR)
    ts(ap("s8I"), ap("pI"), 8, ADD); ts(ap("s8I"), ap("s8I"), 15, AND)
    for a, b in (("pF", "pI"), ("sF", "sI"), ("gF", "gI"), ("s8F", "s8I"), ("s2F", "s2I")):
        cp(ap(a), ap(b))
    ts(ap("sge8"), ap("sF"), 7.5, GT); ts(ap("slt8"), ap("sF"), 7.5, LT)
    ts(ap("CS"), ap("IC"), 15, AND); ts(ap("CG"), ap("IC"), 4, SHR); ts(ap("C3"), ap("IC", 0, 128), 3, AND)
    ts(ap("BLKB"), ap("CG", 0, 128), ap("gF"), EQ); cp(ap("BLKH"), ap("BLKB"))
    r8 = slice(0, 8)
    ts(ap("REP8"), ap("CG", 0, 128, 1, r8), ap("pF", 0, 1, 1, r8), EQ)
    ts(ap("tmpA"), ap("C3"), 1.0, ADD); tt(ap("tmpB"), ap("tmpA"), ap("BLKB"), MUL); ts(ap("CQB"), ap("tmpB"), -1.0, ADD)
    ts(ap("tmpA"), ap("CS", 0, 128), 1.0, ADD); tt(ap("tmpB"), ap("tmpA"), ap("BLKB"), MUL); ts(ap("CSB"), ap("tmpB"), -1.0, ADD)
    ts(ap("PH"), ap("CSB"), ap("s8F"), EQ)
    ts(ap("PL"), ap("CSB"), ap("s8F"), EQ, ap("sge8"), MUL); ts(ap("PR"), ap("CSB"), ap("s8F"), EQ, ap("slt8"), MUL)
    cp(ap("hwf"), ap("hwi")); ts(ap("hwg"), ap("hwf"), 2047.5, GT, -4096.0, MUL); tt(ap("hwg"), ap("hwf"), ap("hwg"), ADD); cp(ap("hwh"), ap("hwg"))
    mm([(ap("MS", 0, 2), ap("PH"), ap("hwh"), True, True)])
    cp(ap("ws"), ap("MS", 0, 2)); ts(ap("wl"), ap("ws"), ap("sge8"), MUL); ts(ap("wr"), ap("ws"), ap("slt8"), MUL)

    def wt(k, qv, r):
        i = (k * 2 + qv) * 4 + r
        return ap("WT", i * 128, i * 128 + 128)
    ts(ap("rsc"), ap("slt8"), -1.0, MUL)
    for r in (1, 2, 3):
        ts(ap("rs%d" % r), ap("rsc"), float(r), ADD)
    for qv in (0, 1):
        ts(wt(0, qv, 0), ap("CQB"), 0.0, EQ, ap("wl", qv, qv + 1), MUL)
        for r in (1, 2, 3):
            ts(wt(0, qv, r), ap("CQB"), ap("rs%d" % r), EQ, ap("ws", qv, qv + 1), MUL)
        ts(wt(1, qv, 3), ap("CQB"), 3.0, EQ, ap("wr", qv, qv + 1), MUL)
    for qv in (0, 1):
        for r in range(4):
            ts(wt(2, qv, r), ap("CQB"), float(r), EQ, ap("hwg", qv, qv + 1), MUL)
    ts(ap("MQ"), ap("C3"), ap("s2F"), EQ)
    ts(ap("MWR"), ap("CS"), ap("sF"), EQ); ts(ap("RST"), ap("CS"), 0.5, GT)
    ts(ap("ksc"), ap("kmi"), -2048.0, ADD); ts(ap("kh"), ap("CS", 0, 16), ap("sF"), EQ, ap("ksc"), MUL)
    mm([(ap("MS", 16, 32), ap("BLKH"), ap("kh"), True, True)])
    ts(ap("KR"), ap("MS", 16, 32), 2048.0, ADD)
    ts(ap("th8h"), ap("th8"), -2048.0, ADD)
    mm([(ap("MS", 8, 9), ap("REP8"), ap("th8h"), True, True)])
    ts(ap("th16"), ap("MS", 8, 9), 2048.0 - 1.0 / 512, ADD, 512.0, MUL)
    ts(ap("c8h"), ap("c8"), -2048.0, ADD)
    mm([(ap("HR", 0, 256), ap("REP8"), ap("c8h"), True, True)])
    act(ap("CX0", 0, 256), ap("HR", 0, 256), AF.Copy, bias=2048.0)
    tt(ap("CM"), ap("CX0", 0, 256), ap("MWR"), MUL); scan(ap("CM2"), ap("RST"), ap("CM")); cp(ap("CL0"), ap("CM2", 15, 256, 16))
    for k in "01":
        fill(ap("TX" + k, 256, 640), 0.0)
    act(ap("TX0", 0, 256), ind(ap("TP"), ap("CL0")), AF.Copy)
    act(ap("BLK8"), ap("BLKB"), AF.Copy, scale=8192.0);
    ts(ap("NM"), ap("CS"), ap("sF"), NE, 4194304.0, MUL); ts(ap("RSTB"), ap("CS"), 0.5, LT, 8388608.0, MUL)
    act(ap("B512"), ap("BLKB"), AF.Copy, scale=512.0); act(ap("B256"), ap("BLKB"), AF.Copy, scale=16.0)


    def keep(o, src, pattern, base):
        put("G", lambda g: g.affine_select(res(o), res(ap(src)), pattern, EQ, 0.0, base, 0), [ap(src)], [o], 0.4)
    for r in range(8):
        keep(ap("SLP", 128 * r, 128 * r + 128), "B512", [[0, 16], [1, 8]], -r)
    slp = len(ops) - 1
    for s in range(16):
        keep(ap("SEL", 128 * s, 128 * s + 128), "B256", [[0, 8], [1, 16]], -s); later(slp)
    slp = len(ops) - 1
    for r in range(4):
        keep(ap("SLQ", 128 * r, 128 * r + 128), "B512", [[0, 32], [1, 4]], -r); later(slp)
    slp = len(ops) - 1
    put("G", lambda g: g.iota(res(ap("WTAB")), [[0, 1024], [1, 4]], 4, 0, allow_small_or_imprecise_dtypes=True), [], [ap("WTAB")], 7.0); later(slp)
    cp(ap("CI"), ap("CX0", 0, 256)); ts(ap("CI3"), ap("CI"), 3, AND); ts(ap("WX0", 0, 256), ap("CI3"), 4.0, ADD)
    ts(ap("W64"), ap("C3", 0, 64), 4.0, ADD)
    ts(ap("s3F"), ap("sF"), 7.5, GT)
    put("G", lambda g: g.iota(res(ap("MP")), [[16, 16], [0, 32]], 0, 0, allow_small_or_imprecise_dtypes=True), [], [ap("MP")], 1.0)
    put("G", lambda g: g.iota(res(ap("ML")), [[16, 16], [4, 4], [0, 4]], 0, 0, allow_small_or_imprecise_dtypes=True), [], [ap("ML")], 0.6)
    ts(ap("k3I"), ap("IC", 0, 64), 1, AND); ts(ap("PZ"), ap("k3I"), ap("s3F"), NE, 4194304.0, MUL)
    ts(ap("PZQ"), ap("C3", 0, 64), ap("s2F"), NE, 4194304.0, MUL)
    ts(ap("CC"), ap("IC", 0, 16), 1.0, MUL); ts(ap("CCL"), ap("IC", 0, 4), 1.0, MUL)
    ts(ap("JW0"), ap("IC", 0, 16), 16.0, MUL, ap("sF"), ADD)
    ts(ap("J256"), ap("JW0"), 256.0, ADD); ts(ap("D4096"), ap("JW0"), 4096.0, ADD)
    ts(ap("FIX", 0, 16), ap("JW0"), 254.5, GT, 256.0, MUL); ts(ap("FIX", 16, 32), ap("JW0"), 253.5, GT, 256.0, MUL)
    ts(ap("CL"), ap("CC"), 16.0, MUL, 15.0, ADD)
    ts(ap("oneR"), ap("CS"), -1.0, GT); ts(ap("EE", 0, 1), ap("pF"), 0.0, MUL)
    ts(ap("tmpA"), ap("CS", 0, 128), ap("sF"), LE, -1.0, MUL); tt(ap("TRIMB"), ap("tmpA"), ap("BLKB"), MUL)
    ts(ap("IDH"), ap("IC", 0, 128), ap("pF"), EQ); cp(ap("IDB"), ap("IDH")); act(ap("ID8"), ap("IDB"), AF.Copy, scale=8192.0); ts(ap("IDN"), ap("IDH"), -1.0, MUL); ts(ap("EQM"), ap("MWR"), -1.0, ADD); fill(ap("ONEB"), 1.0); fill(ap("one16"), 1.0); fill(ap("C255"), 255.0)
    ts(ap("TRP"), ap("CS"), ap("sF"), LE, 16384.0, MUL); ts(ap("TRH"), ap("CS"), ap("sF"), LE, 16384.0, MUL)
    ts(ap("T5"), ap("IC"), 5.0, MUL, 2.0, ADD)
    rng = []
    for c in range(16):
        lo = -((-(64 * c + 2)) // 5); hi = min(256, -((-(112 * c + 110)) // 5))
        rng.append((lo, hi))
    ts(ap("kz1"), ap("IC"), 5.0, MUL, 62.0, ADD); ts(ap("kz1"), ap("kz1"), 6, SHR); ts(ap("kz2"), ap("kz1"), 16.0, MIN)
    ts(ap("kz1"), ap("T5"), -55.5, ADD, 1.0 / 112, MUL); tt(ap("KONST"), ap("kz2"), ap("kz1"), ADD)
    fill(ap("RJ", 0, 16), 300.0)
    ts(ap("IC64"), ap("IC", 0, 64), 1.0, MUL); ts(ap("PF64"), ap("IC64"), 5.0, MUL, 1280.0, ADD)
    fill(ap("HT", 256, 1056), UNF); fill(ap("lHT", 64, 144), UNF); fill(ap("RS", 64, 72), 0.0)

    def sel(bank, o, name, lo, n):
        return [(ap(bank, o, o + n), ap("SEL", 128 * s, 128 * s + 128), ap(name, lo + s, lo + s + 16 * (n - 1) + 1, 16), s == 0, s == 15) for s in range(16)]

    def pair(m):
        return m < 14 and m not in BYS and (m ^ 1) not in BYS

    for t in range(RO):
        start[0] = len(ops)
        cur, nxt = str(t % 2), str(1 - t % 2)
        cx, tx, cy, ty, wx, wy = "CX" + cur, "TX" + cur, "CX" + nxt, "TX" + nxt, "WX" + cur, "WX" + nxt
        last = t == RO - 1
        b16 = ap("th16") if t == 0 else ap("b16a" if t % 2 else "b16b")
        lst = []
        for qv in (0, 1):
            for r in range(4):
                lst.append((ap("UVP", 64 * qv, 64 * qv + 64), wt(0, qv, r), ap(tx, r, r + 253, 4), r == 0, False))
            lst.append((ap("UVP", 64 * qv, 64 * qv + 64), wt(1, qv, 3), ap(tx, 4, 257, 4), False, True))
        mm(lst)
        mm([(ap("ZP", 0, 256), ap("PL"), ap(tx, 0, 256), True, False), (ap("ZP", 0, 256), ap("PR"), ap(tx, 1, 257), False, True)])
        act(ap("ZB", 0, 256), ap("ZP", 0, 256), AF.Copy); act(ap("ZB", 256, 512), ap("ZP", 0, 256), AF.Copy)
        tt(ap("UVM"), ap("UVP", 0, 128), ap("MQ"), MUL)
        tt(ap("UT"), ap("UVM", 0, 128, 2), ap("UVM", 1, 128, 2), ADD)
        tt(ap("UVI"), ap("UT", 0, 64, 2), ap("UT", 1, 64, 2), ADD)
        ts(ap("UVA"), ap("UVI"), 4095, AND)
        tt(ap("UVW"), ap("UVA", 0, 16), ap("UVA", 16, 32), MUL)
        ts(ap("UVA", 16, 32), ap("UVW"), 5, SHR)
        cp(ap("UQ"), ap("UVA"))
        for c in range(16):
            if c % 4 == 3:
                act(ap("HF", c // 4, 64, 4), ap("KR"), AF.Identity, bias=ap("UQ", 16 + c, 17 + c), scale=ap("UQ", c, c + 1))
            else:
                ts(ap("HV", c, 256, 16), ap("KR"), ap("UQ", c, c + 1), MUL, ap("UQ", 16 + c, 17 + c), ADD)
        cp(ap("HV", 3, 256, 4), ap("HF"))
        for h in (0, 1):
            ts(ap("HI", 128 * h, 128 * h + 128), ap("HV", 128 * h, 128 * h + 128), 4095, AND)
            cp(ap("HO", 128 * h, 128 * h + 128), ap("HI", 128 * h, 128 * h + 128))
        for mb in range(4):
            if mb == 0:
                scan(ap("EE", 256, 512), ap("oneR"), ap(wx, 0, 256)); cp(ap("EE", 1, 256), ap("EE", 256, 511))
                mm(sel("MS", 32, "EE", 0, 32))
            for m in range(4 * mb, 4 * mb + 4):
                x, u = ap("X", 256 * m, 256 * m + 256), ind(ap("US", 0, 4096), ap("HO", 16 * m, 16 * m + 16))
                if m in BYS:
                    act(x, u, AF.Copy)
                elif not pair(m):
                    tt(x, u, ap("ZB", 0, 256), SUB)
                    if XCH and m > 2:
                        later(x15)
                    x15 = len(ops) - 1
                elif m % 2 == 0:
                    tt(ap("X", 256 * m, 256 * m + 512), ind(ap("US", 0, 4096), ap("HO", 16 * m, 16 * m + 32)), ap("ZB"), SUB)
                    if XCH and m > 2:
                        later(x15)
                    x15 = len(ops) - 1
            for m in range(4):
                lo = 1024 * mb + 256 * m
                k = 2 if pair(4 * mb + m) else 1
                if k == 2 and m % 2:
                    continue
                if 4 * mb + m in BYS:
                    bank = BYS[4 * mb + m]
                    mm([(ap(bank, 256, 512), ap("IDB"), ap("X", lo, lo + 256), True, False), (ap(bank, 256, 512), ap("IDN"), ap("ZB", 0, 256), False, True)])
                    act(ap("A", lo, lo + 256), ap(bank, 256, 512), AF.Abs)
                else:
                    act(ap("A", lo, lo + 256 * k), ap("X", lo, lo + 256 * k), AF.Abs)
        ts(ap("RM", 0, 64), ap("IC64"), 0.0, MUL, b16, ADD)
        for n, h in enumerate(HB):
            d, lo = ("DA", "DB")[n % 2], 512 * h
            mm([(ap(d, 0, 64), ap("IDB"), ap("MP", 64 * h, 64 * h + 64), True, False), (ap(d, 0, 64), ap("IDB"), ap("PZ"), False, False)] +
               [(ap(d, 0, 64), ap("SLP", 128 * r, 128 * r + 128), ap("A", lo + r, lo + 512, 8), False, r == 7) for r in range(8)])
            tt(ap("RM", 64 * n + 64, 64 * n + 128), ap(d, 0, 64), ap("RM", 64 * n, 64 * n + 64), MIN)
        ts(ap("HT", 0, 256), ap("HI"), -2047.0, ADD); later(x15)
        tt(ap("KQ"), ap("RM", 512, 575, 2), ap("RM", 513, 576, 2), MIN)
        tt(ap("KEY"), ap("KQ", 0, 16), ap("KQ", 16, 32), MIN)
        ts(ap("FI"), ap("MS", 32, 64), 0.2 / 256, MUL); later(x15); ts(ap("EB"), ap("MS", 48, 64), -1.0 / 256, MUL, 0.5, ADD); later(x15)
        ts(ap("FB"), ap("FI"), 256.0, MIN); tt(ap("FC"), ap("FB"), ap("FIX"), MAX)
        tt(ap("NW"), ap("FC", 16, 32), ap("FC", 0, 16), SUB)
        ts(ap("UN0"), ap("NW"), 0.0, EQ, 512.0, MUL); tt(ap("UNC"), ap("UN0"), ap("CC"), ADD)
        if t:
            ts(ind(ap(cx), ap("OBU")), ap("IC64"), 1.0, MUL, float(S + CAP * (t - 1)), ADD); later(x15)
            dma(ext("yc", L * (t - 1), L * t), ap(cx, 0, 256, 1, slice(0, 128, 16)), 2.0)
        fill(ap("ZA", 0, 64), 1024.0)
        ts(ap("PO"), ap("KEY"), b16, GE); tt(ap("PN"), ap("PO"), ap("NW"), MUL); scan(ap("SC"), ap("one16"), ap("PN"))
        scn = len(ops) - 1
        ts(ap("UA"), ap("PN"), 0.5, LT); tt(ap("PEN"), ap("UA"), ap("J256"), MUL)
        pen = len(ops) - 1
        mm([(ap("MS", 64, 80), ap("TRIMB"), ap("PN"), True, False), (ap("MS", 64, 80), ap("BLKB"), ap("SC"), False, False), (ap("MS", 64, 80), ap("IDH"), ap("PEN"), False, True)])
        cp(ap("OF"), ap("MS", 64, 80))
        lender = T.cores[(rank + 1 + t % 3) % 4]
        borrower = T.cores[(rank - 1 - t % 3) % 4]

        def send(o, a, sem, loc, dst):
            rid, pid, se = topo.addr(dst)
            m = 0
            for e in topo.engines(core, dst)[:8]:
                m |= 1 << e
            put("G", lambda g: g.remote_dma(T[o][:, :], res(a), T.sem[sem], T.sem[loc], pid, rid, m), [a], [], 1.0, sem=loc, inc=0)
            ops[-1]["n"] = len(topo.engines(core, dst)[:8])
            put("N", None, [], [ap(o)], FLIGHT, sem=sem, inc=8)
            ops[-1]["after"] = [len(ops) - 2]
        if not last:
            bn = "b16a" if t % 2 == 0 else "b16b"
            mm([(ap("MS", 96, 97), ap("ONEB"), ap("SC", 15, 16), True, True)])
            cp(ap("PPI"), ap("MS", 96, 97)); ts(ap("PPJ"), ap("PPI"), 63, AND); ts(ap(bn), ap("PPJ"), 512.0, MUL, ap("th16"), ADD)
        ts(ap("MI"), ap("KEY"), 511, AND); tt(ap("LD"), ap("MI"), ap("UNC"), ADD); cp(ap("LL"), ap("LD"))
        tt(ap("HM"), ind(ap("HT"), ap("LL")), ap("MWR"), MUL); later(pen); later(scn)
        scan(ap("HS"), ap("RST"), ap("HM"))
        mm([(ap("HR", 0, 256), ap("BLKH"), ap("HM"), True, True)])
        cp(ap("HRH"), ap("HR", 0, 256))
        act(ap(cx, 256, 512), ap("HR", 0, 256), AF.Copy, bias=2047.0)
        ts(ap("HW"), ap("HS", 15, 256, 16), 2047.0, ADD); cp(ap("HL"), ap("HW"))
        mm([(ap("DA", 256, 512), ap("BLKH"), ap("HM"), True, False), (ap("DA", 256, 512), ap("IDH"), ap("TRH"), False, True)])
        act(ap("HRT"), ap("DA", 256, 512), AF.Copy)
        ts(ap("UR"), ap("HRH"), UNF, EQ)
        mm([(ap("CT", 0, 256), ap("ID8"), ap("UR"), True, False), (ap("CT", 0, 256), ap("IDB"), ap("NM"), False, False)])
        for c in range(15):
            ts(ap("ET", 256 * c, 256 * c + 240 - 16 * c), ap("HRH", 16 * c + 16, 256), ap("HS", 16 * c + 15, 16 * c + 16), EQ)
            if c <= NET:
                later(len(ops) - 3)
            mm([(ap("CT", 16 * c + 16, 256), ap("BLK8"), ap("ET", 256 * c, 256 * c + 240 - 16 * c), False, False)])
            if c == max(NET, 0):
                net = len(ops) - 2
                cp(ind(ap("ZA"), ap("OF")), ap("ZB", 0, 256))
                if NET >= 0:
                    later(net)
                send("ZL%d" % t, ap("ZA", 0, 64), "ask%d" % t, "la", lender)
        tt(ap("ET", 3840, 4096), ind(ap("HS"), ap("CL")), ap("HRT"), EQ)
        mm([(ap("CT", 0, 256), ap("BLK8"), ap("ET", 3840, 4096), False, True)])
        ctl = len(ops) - 1
        scan(ap("WS"), ap("RSTB"), ap("CT", 0, 256), ADD, MIN)
        act(ap("WD"), ap("CT", 0, 256), AF.Relu, bias=1.0, scale=-1.0)
        mm([(ap("MS", 256, 512), ap("BLKB"), ap("WD"), True, True)])
        act(ap("WN"), ap("MS", 256, 512), AF.Copy)
        tt(ap("LO1"), ap("WS", 15, 256, 16), ap("HW"), ADD); tt(ap("LO2"), ap("LO1"), ap("D4096"), MIN); cp(ap("LO"), ap("LO2"))
        cp(ind(ap("US"), ap("LO")), ap("C255"))
        zl = "ZL%d" % t
        lst = []
        for qv in (0, 1):
            for r in range(4):
                lst.append((ap("UVP", 128 + 16 * qv, 144 + 16 * qv), wt(2, qv, r), ap(zl, r, r + 61, 4), r == 0, r == 3))
        mm(lst)
        luv = len(ops) - 1
        for k in range(4):
            act(ap("ZT", 64 * k, 64 * k + 64), ap(zl), AF.Copy)
        tt(ap("lUVM"), ap("UVP", 128, 160), ap("MQ", 0, 32), MUL)
        tt(ap("lUT"), ap("lUVM", 0, 32, 2), ap("lUVM", 1, 32, 2), ADD)
        tt(ap("lUVI"), ap("lUT", 0, 16, 2), ap("lUT", 1, 16, 2), ADD)
        ts(ap("lUVA"), ap("lUVI"), 4095, AND)
        tt(ap("lUVW"), ap("lUVA", 0, 4), ap("lUVA", 4, 8), MUL)
        ts(ap("lUVA", 4, 8), ap("lUVW"), 5, SHR)
        cp(ap("lUQ"), ap("lUVA"))
        for c in range(4):
            ts(ap("lHV", c, 64, 4), ap("KR"), ap("lUQ", c, c + 1), MUL, ap("lUQ", 4 + c, 5 + c), ADD)
        ts(ap("lHI"), ap("lHV"), 4095, AND); cp(ap("lHO"), ap("lHI"));
        for mb in range(4):
            w = 256 if mb < 3 else 128
            tt(ap("lX", 256 * mb, 256 * mb + w), ind(ap("US", 0, 4096), ap("lHO", 16 * mb, 16 * mb + w // 16)), ap("ZT", 0, w), SUB)
            lx = len(ops) - 1
        act(ap("lX", 896, 1024), ind(ap("US", 0, 4096), ap("lHO", 56, 64)), AF.Copy)
        mm([(ap("ZP", 256, 384), ap("IDB"), ap("lX", 896, 1024), True, False), (ap("ZP", 256, 384), ap("IDN"), ap("ZT", 0, 128), False, True)])
        ts(ap("lHT", 0, 64), ap("lHI"), -2047.0, ADD); later(lx)
        for mb in range(3):
            act(ap("lA", 256 * mb, 256 * mb + 256), ap("lX", 256 * mb, 256 * mb + 256), AF.Abs)
        act(ap("lA", 896, 1024), ap("ZP", 256, 384), AF.Abs)
        act(ap("lA", 768, 896), ap("lX", 768, 896), AF.Abs)
        ts(ap("lRM", 0, 64), ap("IC64"), 0.0, MUL, b16, ADD)
        for n, h in enumerate((0, 1, 2, 3)):
            d = ("DA", "DB")[n % 2]
            mm([(ap(d, 64, 128), ap("IDB"), ap("ML", 64 * h, 64 * h + 64), True, False), (ap(d, 64, 128), ap("IDB"), ap("PZQ"), False, False)] +
               [(ap(d, 64, 128), ap("SLQ", 128 * r, 128 * r + 128), ap("lA", 256 * h + r, 256 * h + 256, 4), False, r == 3) for r in range(4)])
            tt(ap("lRM", 64 * n + 64, 64 * n + 128), ap(d, 64, 128), ap("lRM", 64 * n, 64 * n + 64), MIN)
        tt(ap("lK1"), ap("lRM", 256, 288), ap("lRM", 288, 320), MIN); tt(ap("lK2"), ap("lK1", 0, 16), ap("lK1", 16, 32), MIN)
        tt(ap("lK3"), ap("lK2", 0, 16, 2), ap("lK2", 1, 16, 2), MIN); tt(ap("lKEY"), ap("lK3", 0, 8, 2), ap("lK3", 1, 8, 2), MIN)
        ts(ap("lMI"), ap("lKEY"), 2, SHR, 127, AND); cp(ap("lLL"), ap("lMI"))
        tt(ap("lHM"), ind(ap("lHT"), ap("lLL")), ap("MWR", 0, 64), MUL)
        scan(ap("lHS"), ap("RST", 0, 64), ap("lHM"))
        mm([(ap("HR", 256, 320), ap("BLKH"), ap("lHM"), True, True)])
        tt(ap("lHRT"), ap("HR", 256, 320), ap("TRP", 0, 64), ADD)
        ts(ap("lHW"), ap("lHS", 15, 64, 16), 2047.0, ADD); tt(ap("lHD"), ap("lHW"), ap("D4096", 0, 4), SUB); cp(ap("lHL"), ap("lHW"))
        ts(ap("lET", 256, 320), ap("HR", 256, 320), UNF, EQ)
        mm([(ap("CT", 256, 320), ap("BLKB"), ap("lET", 256, 320), True, False)])
        for c in range(3):
            ts(ap("lET", 64 * c, 64 * c + 48 - 16 * c), ap("HR", 272 + 16 * c, 320), ap("lHS", 16 * c + 15, 16 * c + 16), EQ)
            mm([(ap("CT", 272 + 16 * c, 320), ap("BLKB"), ap("lET", 64 * c, 64 * c + 48 - 16 * c), False, False)])
        tt(ap("lET", 192, 256), ind(ap("lHS"), ap("CL", 0, 4)), ap("lHRT"), EQ)
        mm([(ap("CT", 256, 320), ap("BLKB"), ap("lET", 192, 256), False, True)])
        lct = len(ops) - 1
        ts(ap("GR"), ap("CT", 256, 320), 0.0, EQ)
        tt(ap("RS", 0, 64), ind(ap("TP"), ap("lHL")), ap("GR"), MUL)
        tt(ap("GM"), ap("CT", 256, 320), ap("EQM", 0, 64), EQ); scan(ap("GS"), ap("RST", 0, 64), ap("GM"))
        ts(ap("RS", 64, 68), ap("GS", 15, 64, 16), -256.0, MUL, 256.0, ADD)
        send("RB%d" % t, ap("RS"), "rep%d" % t, "lr", borrower)
        tt(ap("RSU"), ind(ap("US", 0, 4096), ap("lHL")), ap("GR"), MUL)
        send("RV%d" % t, ap("RSU"), "reu%d" % t, "lu", borrower)
        tt(ap("lO1"), ap("GS", 15, 64, 16), ap("lHD"), MUL); tt(ap("lO2"), ap("lO1"), ap("D4096", 0, 4), ADD); cp(ap("lLO"), ap("lO2"))
        cp(ind(ap("US"), ap("lLO")), ap("C255", 0, 64))
        lend = len(ops) - 1
        mm([(ap("JP", 0, 256), ap("BLKB"), ap("KONST"), True, False)])
        off = 0
        for c in range(16):
            lo, hi = rng[c]
            act(ap("SG", off, off + hi - lo), ap("T5", lo, hi), AF.Sign, bias=ap("EB", c, c + 1))
            mm([(ap("JP", lo, hi), ap("BLKB"), ap("SG", off, off + hi - lo), False, c == 15)])
            off += (hi - lo + 15) // 16 * 16
        act(ap("RJ", 1, 257), ap("JP", 0, 256), AF.Relu, bias=254.0, scale=-0.5)
        mm(sel("JP", 256, "RJ", 1, 16)); later(ctl); later(luv)
        ts(ap("JW"), ap("JP", 256, 272), -1.0 / 256, MUL, 254.0, ADD); later(lx); cp(ap("JL"), ap("JW"))
        mm([(ap("MS", 256, 512), ap("IDB"), ap("RJ", 0, 256), True, False), (ap("MS", 256, 512), ap("IDN"), ap("RJ", 1, 257), False, True)]); later(luv)
        act(ap("FIRST"), ap("MS", 256, 512), AF.Sign)
        tt(ap("FW"), ind(ap("WN"), ap("JL")), ap("FIRST"), MUL); later(lx)
        mm(sel("JP", 272, "FW", 0, 16)); later(lct)
        tt(ap("JX"), ap("JP", 272, 288), ap("JW"), ADD); cp(ap("JL2"), ap("JX"))
        jl2 = len(ops) - 1
        if not last:
            act(ap(tx, 256, 512), ind(ap("TP"), ap("HL")), AF.Copy)
            act(ap(wx, 256, 512), ind(ap("WTAB"), ap("HL")), AF.Copy)
            act(ap(ty, 0, 256), ind(ap(tx, 0, 512), ap("JL2")), AF.Copy)
            act(ap(wy, 0, 256), ind(ap(wx, 0, 512), ap("JL2")), AF.Copy)
        act(ap(cy, 0, 256), ind(ap(cx, 0, 512), ap("JL2")), AF.Copy)
        act(ap("EA", 0, 64), ap("PF64"), AF.Copy)
        cp(ind(ap("EA"), ap("OF")), ap("EE", 0, 256)); later(lend); later(jl2)
        tt(ap("EM"), ap("EA", 0, 64), ap("MWR", 0, 64), MUL); scan(ap("EQ"), ap("RST", 0, 64), ap("EM"))
        ts(ap("FAI"), ap("EQ", 15, 64, 16), 0.2, MUL); cp(ap("FA"), ap("FAI"))
        rb = "RB%d" % t
        tt(ap("OB"), ap(rb, 64, 68), ap("FA"), ADD); cp(ap("OBU"), ap("OB"))
        if not last:
            cp(ind(ap(ty), ap("OBU")), ap(rb, 0, 64)); cp(ind(ap(wy), ap("OBU")), ap("W64"))
        dma(ext("yu", S + CAP * t, S + CAP * t + CAP), ap("RV%d" % t), 2.0)
        if last:
            ts(ind(ap(cy), ap("OBU")), ap("IC64"), 1.0, MUL, float(S + CAP * t), ADD)
            dma(ext("yc", L * t, L * t + L), ap(cy, 0, 256, 1, slice(0, 128, 16)), 2.0)
    dma(ext("yu", 0, S), ap("US", 0, 4096), 6.0)
    return ops


def order(ops, noise=None):
    last = {}
    for i, o in enumerate(ops):
        pre = {}

        def add(j, wait):
            if j != i:
                pre[j] = pre.get(j, False) or wait
        for j in o.get("after", ()):
            pre[j] = False
        for kind in ("R", "W"):
            for nm, lo, hi, st in o[kind]:
                ps = nm in _PS
                for j, k2, lo2, hi2, st2 in last.get(nm, []):
                    same = ops[j]["q"] == o["q"]
                    if ps:
                        if same and o["q"] == "P":
                            add(j, False)
                        elif not same:
                            add(j, True)
                        continue
                    if kind == "R" and k2 == "R":
                        continue
                    if hi <= lo2 or hi2 <= lo or (st == st2 and st > 1 and (lo - lo2) % st):
                        continue
                    add(j, True)
        for kind in ("R", "W"):
            for nm, lo, hi, st in o[kind]:
                ps = nm in _PS
                lst = last.setdefault(nm, [])
                if ps:
                    if lst and ops[lst[-1][0]]["q"] != o["q"]:
                        keep = []
                        other = [e for e in lst if ops[e[0]]["q"] != o["q"]]
                        lst[:] = other[-40:]
                elif kind == "W" and st == 1:
                    lst[:] = [e for e in lst if not (lo <= e[2] and e[3] <= hi) or e[0] == i]
                lst.append((i, kind, lo, hi, st))
        o["pre"] = pre
    n = len(ops)
    succ = [[] for _ in range(n)]
    for i, o in enumerate(ops):
        for j in o["pre"]:
            succ[j].append(i)
    pri = [0.0] * n
    for i in range(n - 1, -1, -1):
        pri[i] = ops[i]["c"] + max([pri[k] + HOP for k in succ[i]], default=0.0)
    if noise is not None:
        pri = [pri[i] + noise[ops[i]["k"]] for i in range(n)]
    left = [len(o["pre"]) for o in ops]
    ready = {}
    est = [0.0] * n
    fin = [0.0] * n
    free = {}
    for i in range(n):
        if left[i] == 0:
            ready.setdefault(ops[i]["q"], []).append(i)
    seq = []
    while len(seq) < n:
        best = None
        for q, lst in ready.items():
            if not lst:
                continue
            f = 0.0 if q == "N" else free.get(q, 0.0)
            m = min(max(f, est[i]) for i in lst)
            c = [i for i in lst if max(f, est[i]) <= m + 0.03]
            b = max(c, key=lambda i: pri[i])
            tm = max(f, est[b])
            h = max((i for i in lst if est[i] <= tm + AHEAD), key=lambda i: pri[i]) if AHEAD else b
            if pri[h] > pri[b] + 0.5 and est[h] > tm and tm + ops[b]["c"] > est[h] + 0.02 and q != "N":
                c = [i for i in lst if max(f, est[i]) + ops[i]["c"] <= est[h] + 0.02]
                b = max(c, key=lambda i: pri[i]) if c else h
                tm = max(f, est[b])
            if best is None or tm < best[0]:
                best = (tm, q, b)
        tm, q, b = best
        ready[q].remove(b)
        o = ops[b]
        o["t"] = tm
        if q == "Y":
            free[q] = tm + 0.1
            fin[b] = tm + o["c"]
        elif q == "N":
            fin[b] = tm + o["c"]
        else:
            free[q] = tm + o["c"]
            fin[b] = tm + o["c"]
        seq.append(b)
        for k in succ[b]:
            left[k] -= 1
            hop = (OWN if ops[k]["q"] == q else HOP) if ops[k]["pre"][b] else 0.0
            est[k] = max(est[k], tm if ops[k]["q"] == q and not ops[k]["pre"][b] else fin[b] + hop)
            if left[k] == 0:
                ready.setdefault(ops[k]["q"], []).append(k)
    return seq, max(fin)


def rank_program(g, core, T, topo):
    rank = T.rank_of(core)
    if rank is None:
        return
    ops = build(rank, core, T, topo)
    seq, _ = order(ops)
    eng = {"V": g.vector, "S": g.scalar, "P": g.tensor, "G": g, "Y": g.sync}
    total = {}
    known = {q: {} for q in eng}
    for i in seq:
        o = ops[i]
        q = o["q"]
        if q == "N":
            o["at"] = (o["sem"], o["inc"]); o["clock"] = {}
            total[o["sem"]] = o["inc"]
            continue
        kn = known[q]
        need = [ops[j] for j, w in o["pre"].items() if w]
        need.sort(key=lambda p: -p.get("t", 0.0))
        for p in need:
            sem, val = p["at"]
            if kn.get(sem, 0) >= val:
                continue
            eng[q].wait_ge(T.sem[sem], val)
            kn[sem] = val
            for a, b in p["clock"].items():
                if kn.get(a, 0) < b:
                    kn[a] = b
        r = o["fn"](g)
        if o["sem"] is None:
            sem = "s" + q
            total[sem] = total.get(sem, 0) + 1
            r.then_inc(T.sem[sem], 1)
        elif "n" in o:
            sem = o["sem"]
            total[sem] = total.get(sem, 0) + o["n"]
        else:
            sem = o["sem"]
            total[sem] = o["inc"]
            r.then_inc(T.sem[sem], o["inc"])
        o["at"] = (sem, total[sem])
        o["clock"] = dict(kn)
    for sem, val in total.items():
        g.wait_ge(T.sem[sem], val)
